import numpy as np, ml_dtypes
CORES = [40,41,42,43,44,45,46,47]
N = 8
BF = ml_dtypes.bfloat16
W, C, M, V, D, Q = 4096, 128, 4, 5, 3, 9
LM = 127
def parts(rng):
    return (rng.integers(0, 256, (N, 8, 16, W)), rng.integers(0, W, (N, 8, 16, C)), rng.integers(0, 256, (N, 8, 16, C)),
            rng.integers(0, 16, (N, 8, 16, 1)), rng.integers(48, 81, (N, 8, 16, 1)))
def pack(x, f, z, w, lm):
    return {"rock": x.reshape(N, 128, W).astype(np.float32).astype(BF), "front": np.ascontiguousarray(f.reshape(N, 128, C)).astype(np.int32),
            "vein": z.reshape(N, 128, C).astype(np.float32).astype(BF), "w": w.reshape(N, 128, 1).astype(np.int32), "lim": lm.reshape(N, 128, 1).astype(np.int32)}
def setup_inputs(rng):
    return pack(*parts(rng))
def setup_inputs_alike(rng):
    x, f, z, w, lm = parts(rng); lm = rng.integers(10, 41, (N, 8, 16, 1)); rec = rng.integers(100, 156, (N, 8, 16, 4))
    x = np.take_along_axis(rec, rng.integers(0, 4, (N, 8, 1, W)), 3)
    far = lm + rng.choice(np.array([-1, 0, 0, 0, 1, 2, 3, 4]), (N, 8, 16, C))
    z = np.take_along_axis(rec, rng.integers(0, 4, (N, 8, 1, C)), 3) + rng.choice(np.array([-1, 1]), (N, 8, 16, C)) * far
    f[:, ::2] = rng.choice(np.array([0, W - 1, W // 2, 3]), (N, 4, 16, C))
    f[:, 1] = f[:, 1][..., rng.integers(0, 4, C)]
    return pack(x, f, z, w, lm)
def setup_inputs_corners(rng):
    x, f, z, w, lm = parts(rng); end = np.array([0, 1, 14, 15]); P = C // 2; h = np.arange(P)
    for a in range(N):
        o = [int(b) for b in rng.permutation(8)]
        for g in range(8):
            v = o[g]
            if v == 0:
                lm[a, g] = 0; w[a, g] = 0
            elif v == 1:
                lm[a, g] = LM; w[a, g] = 15
            elif v in (2, 3, 4):
                x[a, g] = rng.integers(200, 256, (16, W)); z[a, g] = rng.integers(0, 61, (16, C)); lm[a, g] = rng.integers(0, 101, (16, 1))
                s = np.arange(16)[:, None] * (W // 32) + rng.integers(0, W // 32, (16, P)); j = rng.integers(W // 2, W, (16, P))
                if v == 2:
                    k = rng.choice(end, P); l = rng.choice(end, P); k[:16] = np.repeat(end, 4); l[:16] = np.tile(end, 4)
                    s[np.maximum(l, rng.integers(0, 16, P)), h] = s[l, h]
                    j[k, h] = (s[l, h] & -8) + rng.integers(0, 8, P)
                    j[np.maximum(k, rng.integers(0, 16, P)), h] = j[k, h]
                if v == 4:
                    s[:] = W - 1; j[:] = W - 1; s[:, :P // 2] = 0; j[:, :P // 2] = 0
                    s[1:, P // 2:3 * P // 4] = W - 21; j[1:, P // 2:3 * P // 4] = W - 3
                f[a, g][:, 0::2] = s; f[a, g][:, 1::2] = j
            elif v == 5:
                r = rng.integers(64, 192, (16, 1)); x[a, g] = r; lm[a, g] = 0
                off = np.argsort(rng.random((16, C)), axis=0) >= rng.integers(Q - 2, Q + 2, C)[None, :]
                z[a, g] = r + np.where(off, rng.choice(np.array([-40, -4, 4, 40]), (16, C)), 0)
            elif v == 6:
                f[a, g] = (W - 1) * rng.integers(0, 2, (16, C)); w[a, g] = 15 * rng.integers(0, 2, (16, 1)); lm[a, g] = LM * rng.integers(0, 2, (16, 1))
            else:
                w[a, g, 0] = 15; w[a, g, 1] = 1; z[a, g][:, ::2] = 0; z[a, g, 0, ::2] = 136; z[a, g, 1, ::2] = 7; f[a, g][:, ::4] = W - 1
                for i, n, u, m in ((2, W - 3, 2037, 0), (6, W - 15, 2039, 2)):
                    z[a, g, 0, i::8] = 135; z[a, g, 1, i::8] = u - 2025; f[a, g][:, i::8] = n
                    x[a, g][:, (((n * (2 * u + 1)) >> (5 + m)) + n + 613 * m + 37 * np.arange(16)) & (W - 1)] = z[a, g][:, i][:, None]
    return pack(x, f, z, w, lm)
def setup_inputs_ends(rng):
    x, f, z, w, lm = parts(rng)
    x = 255 * np.where(rng.random((N, 8, 1, W)) < 0.4, rng.integers(0, 2, (N, 8, 1, W)), rng.integers(0, 2, (N, 8, 16, W)))
    z = 255 * np.where(rng.random((N, 8, 1, C)) < 0.4, rng.integers(0, 2, (N, 8, 1, C)), rng.integers(0, 2, (N, 8, 16, C)))
    f = (W - 1) * rng.integers(0, 2, f.shape); w = 15 * rng.integers(0, 2, w.shape); lm = LM * rng.integers(0, 2, lm.shape)
    for a, g in ((N - 1, 7), (0, 0)):
        w[a, g] = 15; z[a, g][:, [0, C - 2, C - 1]] = 255; z[a, g][:, [3, C - 3]] = 0
        z[a, g][:, [5, C - 4]] = rng.permutation(np.array([255] * 9 + [26] + [0] * 6))[:, None]
        f[a, g, 15][[0, 3, 5, C - 4, C - 3, C - 2, C - 1]] = W - 1
        for u in ((16 * 15 * 255) & 2047, 0):
            x[a, g][:, ((((W - 1) * (2 * u + 1)) >> (5 + np.arange(M))) + W - 1 + 613 * np.arange(M) + 37 * 15) & (W - 1)] = 0
    return pack(x, f, z, w, lm)
def setup_inputs_full(rng):
    x, f, z, w, lm = parts(rng); P = C // 2; h = np.arange(P); n = W // C
    b = int(rng.integers(0, N)); g = int(rng.integers(0, 8)); rest = [q for q in range(N) if q not in (b, (b - D) % N)]; a = rest[int(rng.integers(0, len(rest)))]
    for q in range(N):
        if q != a:
            x[q, g] = rng.integers(200, 256, (16, W)); z[q, g] = rng.integers(0, 61, (16, C)); lm[q, g] = 0
            f[q, g] = n * rng.permutation(C)[None, :] + rng.integers(0, n, (16, C))
    i = np.array([P - 1, 0, P // 2])[:int(rng.integers(1, 4))]
    f[b, g, 15, 2 * i + 1] = (f[b, g, rng.integers(0, 16, len(i)), 2 * i] & -8) + rng.integers(0, 8, len(i))
    x[a] = rng.integers(200, 256, (8, 16, W)); z[a] = rng.integers(0, 61, (8, 16, C)); lm[a] = rng.integers(80, 121, (8, 16, 1))
    k = rng.integers(0, 16, (8, P)); l = rng.integers(0, 16, (8, P)); gr = np.arange(8)[:, None]; fa = f[a]
    fa[gr, k, 2 * h + 1] = (fa[gr, l, 2 * h] & -8) + rng.integers(0, 8, (8, P))
    o = [int(c) for c in rng.permutation(8)]
    f[a, o[0]] = 0; w[a, o[0]] = 0
    f[a, o[1]] = W - 1; w[a, o[1]] = 0; w[a, o[1], 0] = W >> 9; z[a, o[1], 0] = 32
    return pack(x, f, z, w, lm)
def setup_inputs_spread(rng):
    x = np.minimum((np.exp2(8 * rng.random((N, 8, 1, W))) * rng.random((N, 8, 16, W))).astype(np.int64), 255)
    z = np.minimum((np.exp2(8 * rng.random((N, 8, 1, C))) * rng.random((N, 8, 16, C))).astype(np.int64), 255)
    f = np.minimum((W * rng.random((N, 8, 16, C)) ** 3).astype(np.int64), W - 1)
    return pack(x, f, z, rng.integers(0, 16, (N, 8, 16, 1)), np.minimum((128 * rng.random((N, 8, 16, 1)) ** 2).astype(np.int64), LM))
def check_inputs(d):
    bad = []
    for k, hi in (("rock", 255), ("front", W - 1), ("vein", 255), ("w", 15), ("lim", LM)):
        v = np.asarray(d[k]).astype(np.float64)
        if not (np.min(v) >= 0 and np.max(v) <= hi): bad.append("range of " + k)
        elif np.any(v != np.floor(v)): bad.append("whole numbers in " + k)
    return bad
def reference(rock, front, vein, w, lim):
    x = rock.astype(np.float32).astype(np.int64).reshape(N, 8, 16, W)
    f = front.astype(np.int64).reshape(N, 8, 16, C)
    z = vein.astype(np.float32).astype(np.int64).reshape(N, 8, 16, C)
    wt = w.astype(np.int64).reshape(N, 8, 16, 1); lm = lim.astype(np.int64).reshape(N, 8, 16, 1)
    place = np.arange(16)[:, None]; ci = np.arange(C); met = np.zeros(N, np.int64)
    for t in range(V):
        if t > 0:
            f = np.roll(f, D, axis=0); z = np.roll(z, D, axis=0)
        u = np.add.reduce(wt * z, axis=2) & 2047
        dig = np.add.reduce(z, axis=2) & 15
        top = (lm + (met & 3)[:, None, None, None])[..., None]
        for m in range(M):
            c = (((f * (2 * u[:, :, None, :] + 1)) >> (5 + m)) + f + 613 * m + 37 * place) & (W - 1)
            v = np.take_along_axis(x, c.reshape(N, 8, 1, 16 * C), 3).reshape(N, 8, 16, 16, C)
            dif = np.abs(v - z[:, :, :, None, :])
            score = np.add.reduce(dif, axis=2); near = np.count_nonzero(dif <= top, axis=2)
            if m == 0:
                bs, bc, bn = score, c, near
            else:
                less = score < bs; bs = np.where(less, score, bs); bc = np.where(less, c, bc); bn = np.where(less, near, bn)
        f = np.where(bn >= Q, bc, f)
        sen = ci[((ci >> t) & 1) == 0]; jun = sen + (1 << t)
        fs = f[..., sen]; fj = f[..., jun]
        eq = ((fj[:, :, :, None, :] >> 3) == (fs[:, :, None, :, :] >> 3)).reshape(N, 8, 256, C // 2)
        meet = np.any(eq, axis=2)[:, :, None, :]; first = np.argmax(eq, axis=2)[:, :, None, :]
        k = first >> 4; l = first & 15
        met = np.count_nonzero(meet, axis=(1, 2, 3))
        src = place - l + k
        ns = np.where(meet & (place > l) & (src <= 15), np.take_along_axis(fj, np.minimum(np.maximum(src, 0), 15), 2), fs)
        nj = np.where(meet & (place >= k), (((fj * fs) >> 5) + fj + u[..., jun][:, :, None, :]) & (W - 1), fj)
        f = f.copy(); f[..., sen] = ns; f[..., jun] = nj
        e = np.take_along_axis(f, dig[:, :, None, :], 2)
        old = np.take_along_axis(x, e, 3)
        lo = np.full((N, 8, W), C)
        np.minimum.at(lo, (np.arange(N)[:, None, None], np.arange(8)[None, :, None], e[:, :, 0]), np.broadcast_to(ci, (N, 8, C)))
        zl = np.take_along_axis(z, np.minimum(lo, C - 1)[:, :, None, :], 3)
        x = np.where((lo < C)[:, :, None, :], np.maximum(x - (zl >> 2), 0), x)
        z = (z + old) >> 1
    return {"yx": x.reshape(N, 128, W).astype(np.float32).astype(BF), "yf": f.reshape(N, 128, C).astype(np.float32), "yz": z.reshape(N, 128, C).astype(np.float32).astype(BF)}

@@ -1,0 +1,547 @@
+import math
+from concourse.mybir import AluOpType as A, ActivationFunctionType as AF, AxisListType
+
+NV = 5
+NEARV = ((1, 2, 3), (1, 2, 3))
+SG = (0,)
+ZXV = (16, 0)
+SCRATCH = {
+    "PI": ("sbuf", [128, 8], "int32"), "RF": ("sbuf", [128, 16], "float32"),
+    "ONES": ("sbuf", [128, 160], "bfloat16"), "IEB": ("sbuf", [128, 160], "bfloat16"),
+    "IEH": ("sbuf", [128, 160], "float16"), "I32": ("sbuf", [128, 128], "float32"),
+    "GR": ("sbuf", [128, 128], "float32"), "CR": ("sbuf", [128, 128], "float32"),
+    "XR": ("sbuf", [128, 144], "float32"), "T32": ("sbuf", [128, 128], "float32"),
+    "BLK": ("sbuf", [128, 128], "bfloat16"), "BLH": ("sbuf", [128, 128], "float16"),
+    "R256": ("sbuf", [128, 144], "bfloat16"), "R05": ("sbuf", [128, 144], "bfloat16"), "R1B": ("sbuf", [128, 144], "bfloat16"),
+    "BL16": ("sbuf", [128, 128], "float16"), "MIM": ("sbuf", [128, 128], "float16"), "NI": ("sbuf", [128, 128], "bfloat16"),
+    "C1S": ("sbuf", [128, 4], "float16"), "C32": ("sbuf", [128, 4], "float16"),
+    "LT": ("sbuf", [128, 2, 128], "float16"), "LU": ("sbuf", [128, 2, 128], "float16"),
+    "XG0": ("sbuf", [128, 1024], "bfloat16"), "XG1": ("sbuf", [128, 1024], "bfloat16"),
+    "KM16": ("sbuf", [128, 16], "float32"), "KT": ("sbuf", [128, 16], "float32"),
+    "P4": ("sbuf", [128, 16], "float32"), "P4C": ("sbuf", [128, 1], "float32"),
+    "EL": ("sbuf", [128, 16 * 128], "float16"), "PL": ("sbuf", [128, 16 * 128], "bfloat16"),
+    "SLB": ("sbuf", [128, 128], "bfloat16"), "Q2": ("sbuf", [128, 128], "bfloat16"),
+    "UPI": ("sbuf", [128, 128], "bfloat16"), "S15": ("sbuf", [128, 128], "bfloat16"),
+    "ALLC": ("sbuf", [128, 128], "bfloat16"), "K1": ("sbuf", [128, 2, 256], "bfloat16"),
+    "BB": ("sbuf", [128, 4], "float32"), "PCH": ("sbuf", [128, 2], "float16"),
+    "DUMP": ("sbuf", [128, 8], "float32"), "MK": ("sbuf", [128, 5 * 256], "float16"),
+    "PRW": ("sbuf", [128, 5 * 64], "float32"), "JCI": ("sbuf", [128, 16], "int32"),
+    "PCI": ("sbuf", [128, 5 * 4], "int32"), "PTI": ("sbuf", [128, 5 * 4], "int32"),
+    "PCF": ("sbuf", [128, 5 * 4], "float32"),
+    "W2": ("sbuf", [128, 128], "bfloat16"), "WI": ("sbuf", [128, 2], "int32"),
+    "WF": ("sbuf", [128, 2], "float32"), "LIM": ("sbuf", [128, 1], "float32"),
+    "TOP": ("sbuf", [128, 8], "float32"), "CN": ("sbuf", [128, 4], "float32"), "CI": ("sbuf", [128, 4], "int32"),
+    "FI": ("sbuf", [128, 128], "int32"),
+    "F": ("sbuf", [128, NV * 128], "float32"), "FO": ("sbuf", [128, NV * 128], "float32"),
+    "Z": ("sbuf", [128, NV * 128], "bfloat16"), "ZO": ("sbuf", [128, NV * 128], "bfloat16"),
+    "ROCK": ("sbuf", [128, 4096 + 128], "bfloat16"),
+    "YF": ("sbuf", [128, 128], "float32"), "YZ": ("sbuf", [128, 128], "bfloat16"),
+    "MF": ("sbuf", [128, 128], "float16"), "RN": ("sbuf", [128, 128], "bfloat16"),
+    "OF": ("sbuf", [128, 8], "uint16"), "LO": ("sbuf", [128, 8], "float32"),
+}
+for _n, _w, _d in (("UA", 128, "int32"), ("UI", 64, "int32"), ("SI", 64, "int32"), ("QI", 64, "int32"),
+                   ("HM", 256, "int32"), ("C4", 256, "int32"), ("DN", 256, "float32"),
+                   ("UF", 32, "float32"), ("SM", 64, "float32"), ("ZB", 64, "bfloat16"), ("Z5", 64, "float32"),
+                   ("Z4", 64, "float16"), ("ZZ", 64, "float32"), ("KS", 128, "float32"), ("KM", 128, "float32"),
+                   ("KB", 64, "int32"), ("KC", 64, "int32"), ("PR", 256, "float32"), ("HF", 64, "float16"), ("JC", 32, "float16"),
+                   ("NS", 64, "float32"), ("S2", 64, "float32"), ("EQB", 512, "bfloat16"),
+                   ("PM", 32, "bfloat16"), ("LN", 64, "float32"), ("JM", 32, "bfloat16"), ("XX", 64, "float16"),
+                   ("JG", 32, "float32"), ("CD", 96, "bfloat16"), ("JI", 32, "int32"),
+                   ("JU", 32, "int32"), ("DJ", 32, "float32"), ("FC", 64, "float16"),
+                   ("EF", 8, "float32"), ("SU", 64, "float32"), ("Y1", 64, "int32"), ("RR", 64, "float32"),
+                   ("DU", 512, "bfloat16"), ("OT", 8, "float32"), ("D", 4096, "bfloat16"), ("NR", 4096, "bfloat16")):
+    SCRATCH[_n] = ("sbuf", [128, 2, _w], _d)
+for _h in "01":
+    for _n, _w, _d in (("CO", 256, "uint16"), ("ZX", 1024, "bfloat16"), ("HW", 1024, "float32"), ("LS", 2, "uint16"), ("E16", 4, "uint16")):
+        SCRATCH[_n + _h] = ("sbuf", [128, _w], _d)
+BANKS = ["X0", "X1", "K0", "K1b", "EQ", "HA", "HB", "MM"]
+for _n in BANKS:
+    SCRATCH[_n] = ("psum", [128, 512], "float32")
+
+LOADS = ["wi", "li", "fr", "v0", "v1", "r0", "r1", "r2", "r3"]
+SEMAPHORES = (["sv", "ss", "st", "sg", "sl"] + ["ld_" + n for n in LOADS] + ["od_f", "od_z", "od_x"] +
+              ["ar%s%d%d" % (k, t, h) for k in "fz" for t in range(1, NV) for h in range(2)])
+QSEM = {"v": "sv", "s": "ss", "t": "st", "g": "sg"}
+CYC = 0.00083
+PEC = 0.00045
+LAT = 0.08
+SFIX = 78
+
+
+def add(S, q, cost, reads, writes, fn, sig=None, lat=0.0):
+    i = len(S["ops"])
+    deps = {}
+
+    def dep(j, sem):
+        if j != i:
+            deps[j] = deps.get(j, False) or sem
+    for k in reads + writes:
+        if k in BANKS:
+            for q2, (j, wr) in S["b"].setdefault(k, {}).items():
+                dep(j, q2 != q or (wr and k in reads))
+    for k in reads:
+        if k not in BANKS:
+            for j in S["w"].get(k, []):
+                dep(j, True)
+    for k in writes:
+        if k not in BANKS:
+            for j in S["w"].get(k, []) + S["r"].get(k, []):
+                dep(j, True)
+    for k in reads + writes:
+        if k in BANKS:
+            acc = S["b"][k]
+            acc[q] = (i, k in writes or (q in acc and acc[q][1] and k not in reads))
+        elif k in writes:
+            S["w"][k] = [i]
+            S["r"][k] = []
+    for k in reads:
+        if k not in BANKS and k not in writes:
+            S["r"].setdefault(k, []).append(i)
+    S["ops"].append({"q": q, "cost": cost, "deps": deps, "fn": fn, "sig": sig, "lat": lat, "nm": " ".join(writes)})
+    return i
+
+
+def plan(S):
+    ops = S["ops"]
+    n = len(ops)
+    succ = [[] for _ in range(n)]
+    for i, o in enumerate(ops):
+        for j in o["deps"]:
+            succ[j].append(i)
+    pri = [0.0] * n
+    for i in range(n - 1, -1, -1):
+        o = ops[i]
+        b = 0.0
+        for k in succ[i]:
+            b = max(b, pri[k] + (o["lat"] if o["sig"] else (LAT if ops[k]["deps"][i] else 0.0)))
+        pri[i] = b + o["cost"]
+    left = [len(o["deps"]) for o in ops]
+    ready = {}
+    est = [0.0] * n
+    free = {}
+    for i in range(n):
+        if left[i] == 0:
+            ready.setdefault(ops[i]["q"], []).append(i)
+    order = []
+    end = 0.0
+    while len(order) < n:
+        best = None
+        for q, lst in ready.items():
+            if lst:
+                st = max(free.get(q, 0.0), min(est[i] for i in lst))
+                if best is None or st < best[0]:
+                    best = (st, q)
+        st, q = best
+        lst = ready[q]
+        c = max((i for i in lst if est[i] <= st + 1e-9), key=lambda i: (pri[i], -i))
+        for i in lst:
+            if pri[i] > pri[c] and est[i] < st + 0.5 * ops[c]["cost"]:
+                c = i
+        st = max(st, est[c])
+        lst.remove(c)
+        o = ops[c]
+        fin = st + o["cost"]
+        free[q] = fin
+        o["start"] = st
+        end = max(end, fin + o["lat"])
+        order.append(c)
+        for k in succ[c]:
+            d = ops[k]["deps"][c]
+            l = o["lat"] if o["sig"] else (LAT if d else 0.0)
+            est[k] = max(est[k], fin + l if d else st)
+            left[k] -= 1
+            if left[k] == 0:
+                ready.setdefault(ops[k]["q"], []).append(k)
+    S["end"] = end
+    return order
+
+
+def issue(S, order, eng, T):
+    ops = S["ops"]
+    cnt = {}
+    known = {q: {} for q in eng}
+    for i in order:
+        o = ops[i]
+        q = o["q"]
+        kn = known[q]
+        need = {}
+        for j, sem in o["deps"].items():
+            if sem:
+                s, val = ops[j]["done"]
+                if kn.get(s, 0) < val:
+                    need[s] = max(need.get(s, 0), val)
+        for s in sorted(need):
+            eng[q].wait_ge(T.sem[s], need[s])
+        for j, sem in o["deps"].items():
+            if sem:
+                for s, val in ops[j]["clock"].items():
+                    if kn.get(s, 0) < val:
+                        kn[s] = val
+        if o["sig"]:
+            o["fn"]()
+            o["done"] = o["sig"]
+        else:
+            s = QSEM[q]
+            cnt[s] = cnt.get(s, 0) + 1
+            o["fn"]().then_inc(T.sem[s], 1)
+            o["done"] = (s, cnt[s])
+        o["clock"] = dict(kn)
+        o["clock"][o["done"][0]] = o["done"][1]
+    return cnt
+
+
+def record(g, core, T, topo):
+    rank = T.rank_of(core)
+    S = {"ops": [], "w": {}, "r": {}, "b": {}, "sends": 0}
+    v, sc, te = g.vector, g.scalar, g.tensor
+
+    def seq(calls):
+        def fn():
+            for c in calls:
+                x = c()
+            return x
+        return fn
+
+    def V(cyc, R, W, *calls):
+        return add(S, "v", max(cyc, 64 * len(calls)) * CYC, R, W, seq(calls))
+
+    def SC(cyc, R, W, *calls):
+        return add(S, "s", (cyc + SFIX * len(calls)) * CYC, R, W, seq(calls))
+
+    def PE(cyc, R, W, mms):
+        return add(S, "t", cyc * PEC, R, W, seq([(lambda m: lambda: te.matmul(*m))(m) for m in mms]))
+
+    def G(cost, R, W, call):
+        return add(S, "g", cost, R, W, call)
+
+    def ts(out, in0, s1, s2, op0, op1=None):
+        if op1 is None:
+            return lambda: v.tensor_scalar(out, in0, s1, None, op0)
+        return lambda: v.tensor_scalar(out, in0, s1, s2, op0, op1)
+
+    def tt(out, a, b, op):
+        return lambda: v.tensor_tensor(out, a, b, op)
+
+    def cp(out, a):
+        return lambda: v.tensor_copy(out, a)
+
+    def ac(out, a, f, **kw):
+        return lambda: sc.activation(out, a, f, **kw)
+
+    def ms(ap, c):
+        return lambda: v.memset(ap, c)
+
+    def load(q, name, out, in_, W, lat):
+        e = g.sync if q == "y" else g.scalar
+        add(S, q, 0.06, [], W, lambda: e.dma_start(out, in_).then_inc(T.sem["ld_" + name], 16), ("ld_" + name, 16), lat)
+
+    load("y", "fr", T.FI[:], T.front[:], ["FI"], 2.2)
+    load("s", "v0", T.Z[:, 0:64], T.vein[:, 0:64], ["Z00"], 2.2)
+    load("y", "wi", T.WI[:, 0:1], T.w[:], ["WI0"], 2.2)
+    load("y", "li", T.WI[:, 1:2], T.lim[:], ["WI1"], 2.2)
+    load("s", "v1", T.Z[:, 64:128], T.vein[:, 64:128], ["Z01"], 2.2)
+    for b in range(4):
+        load("y", "r%d" % b, T.ROCK[:, 1024 * b:1024 * b + 1024], T.rock[:, 1024 * b:1024 * b + 1024], ["ROCK%d" % b], 5.0)
+    RK = ["ROCK%d" % b for b in range(4)]
+
+    def ioF(ap, pat, base, cm):
+        return lambda: g.iota(ap, pat, base, cm, allow_small_or_imprecise_dtypes=True)
+
+    def ioI(ap, pat, base, cm):
+        return lambda: g.iota(ap, pat, base, cm)
+    G(0.15, [], ["PI"], ioI(T.PI[:, 0:1], [[1, 1]], 0, 1))
+    G(0.35, [], ["GR"], ioF(T.GR[:], [[1, 8], [0, 16]], 0, 0))
+    G(0.35, [], ["XR"], ioF(T.XR[:, 0:143], [[1, 143]], -15, 0))
+    V(64, [], ["ONES"], ms(T.ONES[:], 1.0))
+    G(0.45, ["ONES"], ["IEB"], lambda: g.affine_select(T.IEB[:, 0:158], T.ONES[:, 0:158], [[-1, 158]], A.is_equal, 0.0, 15, 1))
+    G(0.35, [], ["CR"], ioF(T.CR[:], [[0, 8], [1, 16]], 0, 0))
+    G(0.2, [], ["KM0"], ioF(T.KM16[:], [[1, 16]], 0, 0))
+    V(64, ["PI"], ["PIr"], ts(T.PI[:, 1:2], T.PI[:, 0:1], 15, None, A.bitwise_and))
+    V(64, ["PI"], ["PIg"], ts(T.PI[:, 2:3], T.PI[:, 0:1], 4, None, A.arith_shift_right))
+    V(64, ["PIr"], ["r"], cp(T.RF[:, 0:1], T.PI[:, 1:2]))
+    V(64, ["PIg"], ["gp"], cp(T.RF[:, 1:2], T.PI[:, 2:3]))
+    r = T.RF[:, 0:1]
+    gp = T.RF[:, 1:2]
+    V(64, ["gp"], ["gp16"], ts(T.RF[:, 2:3], gp, 16.0, None, A.mult))
+    V(128, ["GR", "gp"], ["BLK"], ts(T.BLK[:], T.GR[:], gp, None, A.is_equal))
+    V(64, ["BLK"], ["BLH"], cp(T.BLH[:], T.BLK[:]))
+    V(64, ["WI0"], ["WF0"], ts(T.WF[:, 0:1], T.WI[:, 0:1], 2.0, None, A.mult))
+    V(64, ["WI1"], ["LIM"], ts(T.LIM[:], T.WI[:, 1:2], 0.5, None, A.add))
+    V(64, ["LIM"], ["TOP0"], cp(T.TOP[:, 0:1], T.LIM[:]))
+    V(64, ["BLK", "WF0"], ["W2"], ts(T.W2[:], T.BLK[:], T.WF[:, 0:1], None, A.mult))
+    V(128, ["FI"], ["F00", "F01"], cp(T.F[:, 0:128], T.FI[:]))
+    V(4 * 64, ["r"], ["BB"], *[ts(T.BB[:, m:m + 1], r, 37.0 * 2 ** (4 + m), 613.0 * m * 2 ** (4 + m), A.mult, A.add) for m in range(4)])
+    V(64, ["r"], ["c1"], ts(T.RF[:, 4:5], r, -1.0, 1039.0, A.mult, A.add))
+    V(64, ["r"], ["c2"], ts(T.RF[:, 5:6], r, -1.0, 1054.0, A.mult, A.add))
+    V(64, ["PIr"], ["PIs"], ts(T.PI[:, 3:4], T.PI[:, 1:2], 1.0, None, A.add))
+    V(64, ["PIs"], ["PIt"], ts(T.PI[:, 4:5], T.PI[:, 3:4], 15, None, A.bitwise_and))
+    V(64, ["PIt"], ["rp1"], cp(T.RF[:, 3:4], T.PI[:, 4:5]))
+    V(64, [], ["q25"], ms(T.RF[:, 6:7], 0.25))
+    V(64, ["BLH"], ["BL16"], ts(T.BL16[:], T.BLH[:], 0.0625, None, A.mult))
+    V(128, ["CR", "r"], ["MIM"], ts(T.MIM[:], T.CR[:], r, None, A.is_equal))
+    V(64, ["KM0", "gp"], ["C1S"], ts(T.C1S[:], T.KM16[:, 0:4], gp, None, A.is_equal))
+    V(64, ["C1S"], ["C32"], ts(T.C32[:], T.C1S[:], 32.0, None, A.mult))
+    V(64, ["IEB"], ["NI"], ts(T.NI[:], T.IEB[:, 15:143], -1.0, None, A.mult))
+    for n, c in (("R256", 256.0), ("R05", 0.5), ("R1B", 1.0)):
+        V(143, ["XR", "gp16"], [n], ts(T[n][:, 0:143], T.XR[:, 0:143], T.RF[:, 2:3], c, A.is_equal, A.mult))
+    V(64, [], ["ALLC"], ms(T.ALLC[:], 1.0 / 128))
+    V(512, [], ["K1"], *[ms(T.K1[:, h, 64 * m:64 * m + 64], 64.0 * m + (23 if m in NEARV[h] else 31)) for m in range(4) for h in range(2)])
+    V(80, ["IEB"], ["IEH"], cp(T.IEH[:, 0:158], T.IEB[:, 0:158]))
+    V(128, ["IEB"], ["I32"], cp(T.I32[:], T.IEB[:, 15:143]))
+    V(64, ["KM0", "r"], ["KT"], ts(T.KT[:], T.KM16[:], r, None, A.is_equal))
+    V(64, ["KT"], ["KM0"], ts(T.KM16[:], T.KT[:], -1.0, None, A.mult))
+    V(16 * 64, ["BLK", "KM0"], ["EL"], *[ts(T.EL[:, 128 * l:128 * l + 128], T.BLK[:], T.KM16[:, l:l + 1], None, A.mult) for l in range(16)])
+    V(16 * 64, [], ["P4"], *[ms(T.P4[:, l:l + 1], 4.0 ** l) for l in range(16)])
+    V(64, ["P4", "KT"], ["P4b"], tt(T.P4[:], T.P4[:], T.KT[:], A.mult))
+    V(64, ["P4b"], ["P4C"], lambda: v.tensor_reduce(T.P4C[:], T.P4[:], AxisListType.X, A.add))
+    V(64, ["BLK", "P4C"], ["Q2"], ts(T.Q2[:], T.BLK[:], T.P4C[:, 0:1], None, A.mult))
+    V(128, ["CR", "r"], ["T32"], ts(T.T32[:], T.CR[:], r, -(2.0 ** 40), A.is_gt, A.mult))
+    V(256, ["T32", "BLK"], ["SLB"], tt(T.SLB[:], T.T32[:], T.BLK[:], A.mult))
+    for l in range(16):
+        G(0.4, ["SLB"], ["PL%d" % l], (lambda l: lambda: g.affine_select(T.PL[:, 128 * l:128 * l + 128], T.SLB[:], [[-1, 128]], A.not_equal, 4.0 ** (15 - l), 0, 1))(l))
+    V(128, ["CR", "r"], ["T32"], ts(T.T32[:], T.CR[:], r, None, A.is_ge))
+    V(256, ["T32", "BLK"], ["UPI"], tt(T.UPI[:], T.T32[:], T.BLK[:], A.mult))
+    V(64, ["ONES", "KT"], ["S15"], ts(T.S15[:], T.ONES[:, 0:128], T.KT[:, 15:16], None, A.mult))
+    G(0.2, [], ["JCI0"], ioI(T.JCI[:, 0:8], [[16, 8]], 0, 0))
+    V(64, ["JCI0", "r"], ["JCI1"], ts(T.JCI[:, 8:16], T.JCI[:, 0:8], r, None, A.add))
+    V(64, ["JCI1"], ["PCH"], cp(T.PCH[:], T.JCI[:, 8:10]))
+    V(64, ["JCI1"], ["DUMP"], ts(T.DUMP[:], T.JCI[:, 8:16], 4096.0, None, A.add))
+    V(128, [], ["HWz0", "HWz1"], ms(T.HW0[:, 0:32], 0.0), ms(T.HW1[:, 0:32], 0.0))
+    for t in range(NV):
+        a = t + 1
+        G(0.25, [], ["PRW%d" % t], ioF(T.PRW[:, 64 * t:64 * t + 64], [[1, 2 ** a], [2 ** a, 2 ** (6 - a)]], 0, 0))
+        pc, pt, pf = T.PCI[:, 4 * t:4 * t + 4], T.PTI[:, 4 * t:4 * t + 4], T.PCF[:, 4 * t:4 * t + 4]
+        V(64, ["JCI1"], ["PCI%d" % t], ts(pc, T.JCI[:, 8:12], 2 ** (6 - a) - 1, None, A.bitwise_and))
+        V(64, ["JCI1"], ["PTI%d" % t], ts(pt, T.JCI[:, 8:12], 6 - a, None, A.arith_shift_right))
+        V(64, ["PCI%d" % t], ["PCF%d" % t], ts(pf, pc, float(2 ** a), None, A.mult))
+        V(64, ["PCF%d" % t, "PTI%d" % t], ["PCG%d" % t], tt(pf, pf, pt, A.add))
+        V(256, ["PRW%d" % t, "PCG%d" % t], ["MK%d" % t],
+          *[ts(T.MK[:, 256 * t + 64 * c:256 * t + 64 * c + 64], T.PRW[:, 64 * t:64 * t + 64], T.PCF[:, 4 * t + c:4 * t + c + 1], 8192.0, A.is_ge, A.mult) for c in range(4)])
+    SC(0, ["q25"], ["lnw"], ac(T.RF[:, 7:8], T.RF[:, 6:7], AF.Ln))
+
+    MM, EQ = T.MM, T.EQ
+    IH = T.IEH[:, 15:143]
+    PLK = ["PL%d" % l for l in range(16)]
+
+    def claims(t, h):
+        k, H, xk = "%d%d" % (t, h), str(h), "X%d" % h
+        o = (2 * t + h) * 64
+        F, Z, X = T.F[:, o:o + 64], T.Z[:, o:o + 64], T[xk]
+        CO, ZX = T["CO" + H], T["ZX" + H]
+        nX = X[:, 384:448]
+        SC(5 * 64, ["F" + k, "BB"], [xk], ac(nX, F, AF.Copy),
+           *[ac(X[:, 128 + 64 * m:192 + 64 * m], F, AF.Identity, bias=T.BB[:, m:m + 1], scale=float(2 ** (4 + m))) for m in range(4)])
+        PE(128, ["Z" + k, "W2", "BLK"], [xk], [(X[:, 0:64], T.W2[:], Z, True, True), (X[:, 64:128], T.BLK[:], Z, True, True)])
+        hh, u1 = T.UA[:, h, 0:64], T.UI[:, h, :]
+        V(128, [xk], ["UA" + H], ts(T.UA[:, h, :], X[:, 0:128], 1.0, None, A.add))
+        V(64, ["UA" + H], ["UI" + H], ts(u1, hh, 4095, None, A.bitwise_and))
+        V(64, [xk, "UI" + H], ["QI" + H], tt(T.QI[:, h, :], nX, u1, A.mult))
+        V(64, ["QI" + H], ["UAh" + H], ts(hh, T.QI[:, h, :], 1, None, A.arith_shift_right))
+        V(256, [xk, "UAh" + H], ["HM" + H], *[tt(T.HM[:, h, 64 * m:64 * m + 64], X[:, 128 + 64 * m:192 + 64 * m], hh, A.add) for m in range(4)])
+        V(256, ["HM" + H], ["C4" + H], *[ts(T.C4[:, h, 64 * m:64 * m + 64], T.HM[:, h, 64 * m:64 * m + 64], 4 + m, 4095, A.arith_shift_right, A.bitwise_and) for m in range(4)])
+        V(256, ["C4" + H], ["CO" + H], cp(CO[:], T.C4[:, h, :]))
+        for b in range(0, 16, 4):
+            if b < ZXV[h]:
+                V(256, ["Z" + k], ["ZX%s%d" % (H, b)], *[cp(ZX[:, p:1024:16], Z) for p in range(b, b + 4)])
+            else:
+                SC(256, ["Z" + k], ["ZX%s%d" % (H, b)], *[ac(ZX[:, p:1024:16], Z, AF.Copy) for p in range(b, b + 4)])
+        V(64, ["UA" + H], ["SI" + H], ts(T.SI[:, h, :], T.UA[:, h, 64:128], 15, None, A.bitwise_and))
+        V(256, [xk, "C4" + H], ["DN" + H], *[tt(T.DN[:, h, 64 * m:64 * m + 64], T.C4[:, h, 64 * m:64 * m + 64], nX, A.subtract) for m in range(4)])
+        PE(256, ["F" + k, "I32"], [xk], [(X[:, 448:512], T.I32[:], F, True, False)])
+        V(64, ["UI" + H], ["UF" + H], ts(T.UF[:, h, :], T.UI[:, h, 1:64:2], -1.0, 0.5, A.add, A.mult))
+        V(128, ["SI" + H, "rp1"], ["SM" + H], *[ts(T.SM[:, h, 32 * b:32 * b + 32], T.SI[:, h, b:64:2], T.RF[:, 3:4], None, A.is_equal) for b in range(2)])
+        zb = T.ZB[:, h, :]
+        SC(64, ["Z" + k], ["ZB" + H], *[ac(T.ZB[:, h, 32 * b:32 * b + 32], T.Z[:, o + b:o + 64:2], AF.Copy) for b in range(2)])
+        SC(64, ["ZB" + H], ["Z5" + H], ac(T.Z5[:, h, :], zb, AF.Copy, bias=-0.5))
+        V(64, ["ZB" + H], ["Z4" + H], ts(T.Z4[:, h, :], zb, 0.25, 1025 - 0.375, A.mult, A.add))
+        V(128, ["ZB" + H, "Z4" + H], ["ZZ" + H], tt(T.ZZ[:, h, :], T.Z4[:, h, :], zb, A.add))
+
+    def moves(t, h):
+        k, H = "%d%d" % (t, h), str(h)
+        kk = BANKS[2 + h]
+        KK = T[kk]
+        CO, ZX = T["CO" + H], T["ZX" + H]
+        o = (2 * t + h) * 64
+        PE(256, ["ALLC", "K1"], [kk], [(KK[:, 0:256], T.ALLC[:], T.K1[:, h, :], True, False)])
+        for m in range(4):
+            d, n = "D%d%d" % (h, m), "N%d%d" % (h, m)
+            dm, nm = T.D[:, h, 1024 * m:1024 * m + 1024], T.NR[:, h, 1024 * m:1024 * m + 1024]
+            zk = ["ZX%s%d" % (H, b) for b in range(0, 16, 4)]
+            win = T.ROCK[:, 0:4096].indirect(CO[:, 64 * m:64 * m + 64])
+            if m in SG:
+                xg = T["XG" + H]
+                SC(1536, RK + ["CO" + H], ["XG" + H], ac(xg[:], win, AF.Copy))
+                for b, bk in ((0, "HA"), (1, "HB")):
+                    PE(1024, ["XG" + H, "IEB", "NI"] + zk, [bk], [(T[bk][:], T.IEB[:, 15:143], xg[:, 512 * b:512 * b + 512], True, False),
+                                                                (T[bk][:], T.NI[:], ZX[:, 512 * b:512 * b + 512], False, True)])
+                    SC(512, [bk], [d + "ab"[b]], ac(T.D[:, h, 1024 * m + 512 * b:1024 * m + 512 * b + 512], T[bk][:], AF.Abs))
+            else:
+                V(60 + 1536, RK + ["CO" + H] + zk, [d + "a", d + "b"], tt(dm, win, ZX[:], A.subtract))
+                SC(1024, [d + "a", d + "b"], [d + "a", d + "b"], ac(dm, dm, AF.Abs))
+            if m in NEARV[h]:
+                V(512, [d + "a", d + "b", "TOP%d" % t], [n + "a", n + "b"], ts(nm, dm, T.TOP[:, t:t + 1], None, A.is_le))
+            else:
+                SC(1024, [d + "a", d + "b", "TOP%d" % t], [n + "a", n + "b"], ac(nm, dm, AF.Sign, bias=T.TOP[:, t:t + 1], scale=-1.0))
+
+        def keys(m, near):
+            w, src, b = (("R1B" if m in NEARV[h] else "R05"), T.NR, "N") if near else ("R256", T.D, "D")
+            PE(1024, ["%s%d%d%s" % (b, h, m, x) for x in "ab"] + [w], [kk], [(KK[:, 64 * m:64 * m + 64], T[w][:, 15 - p:143 - p], src[:, h, 1024 * m + p:1024 * m + 1024:16], False, near and m == 3 and p == 15) for p in range(16)])
+        for m, near in ((0, 0), (1, 0), (0, 1), (2, 0), (1, 1), (3, 0), (2, 1), (3, 1)):
+            keys(m, bool(near))
+        V(128, [kk], ["KS" + H], cp(T.KS[:, h, :], KK[:, 128:256]))
+        V(128, [kk, "KS" + H], ["KM" + H], tt(T.KM[:, h, :], KK[:, 0:128], T.KS[:, h, :], A.min))
+        V(128, ["KM" + H], ["KB" + H], tt(T.KB[:, h, :], T.KM[:, h, 0:64], T.KM[:, h, 64:128], A.min))
+        V(64, ["KB" + H], ["KC" + H], ts(T.KC[:, h, :], T.KB[:, h, :], 255, 5, A.bitwise_and, A.arith_shift_right))
+        V(256, ["KC" + H], [kk], *[ts(KK[:, 256 + 64 * m:320 + 64 * m], T.KC[:, h, :], float(2 * m + 1), None, A.is_equal) for m in range(4)])
+        V(256, [kk, "DN" + H], ["PR" + H], tt(T.PR[:, h, :], KK[:, 256:512], T.DN[:, h, :], A.mult))
+        X = T["X" + H]
+        PE(4 * 256, ["PR" + H, "I32"], ["X" + H], [(X[:, 448:512], T.I32[:], T.PR[:, h, 64 * m:64 * m + 64], False, m == 3) for m in range(4)])
+
+    def meetings(t, h):
+        k, H = "%d%d" % (t, h), str(h)
+        o = (2 * t + h) * 64
+        kk, xk = BANKS[2 + h], "X" + H
+        KK, NP = T[kk], T[xk][:, 448:512]
+        HW, LS, FO = T["HW" + H], T["LS" + H], T.FO
+        SS, JJ = T.NS[:, h, 0:64:2], T.NS[:, h, 1:64:2]
+        V(64, [xk], ["HF" + H], ts(T.HF[:, h, :], NP, 0.125, 1025 - 0.4375, A.mult, A.add))
+        V(64, [xk], ["JC" + H], ts(T.JC[:, h, :], T[xk][:, 449:512:2], -2048.0, None, A.add))
+        SC(64, [xk], ["NS" + H], ac(T.NS[:, h, :], NP, AF.Copy))
+        SC(64, ["NS" + H], ["S2" + H], ac(T.S2[:, h, :], T.NS[:, h, :], AF.Copy, bias=-2048.0))
+        for b, bk in ((0, "EQ"), (1, "MM")):
+            mm = []
+            for l in range(8):
+                dd = T[bk][:, 32 * l:32 * l + 32]
+                mm.append((dd, IH, T.HF[:, h, 1:64:2], True, False))
+                mm.append((dd, T.EL[:, 128 * (8 * b + l):128 * (8 * b + l) + 128], T.HF[:, h, 0:64:2], False, True))
+            PE(16 * 64, ["HF" + H, "EL", "IEH"], [bk], mm)
+            V(256, [bk], ["EQB%s%d" % (H, b)], ts(T.EQB[:, h, 256 * b:256 * b + 256], T[bk][:, 0:256], 0.0, None, A.is_equal))
+            PE(512, ["EQB%s%d" % (H, b)] + PLK, [kk], [(KK[:, 256:288], T.PL[:, 128 * l:128 * l + 128], T.EQB[:, h, 32 * l:32 * l + 32], l == 0, l == 15) for l in range(8 * b, 8 * b + 8)])
+        jc, pm = T.JC[:, h, :], T.PM[:, h, :]
+        PE(15 * 64, ["JC" + H, "IEH"], ["HA"], [(T.HA[:, 32 * s:32 * s + 32], T.IEH[:, s - 1:s + 127], jc, True, True) for s in range(1, 16)])
+        PE(16 * 64, ["JC" + H, "IEH"], ["HB"], [(T.HB[:, 32 * s - 512:32 * s - 480], T.IEH[:, s - 1:s + 127], jc, True, True) for s in range(16, 32)])
+        V(64, [kk], ["PM" + H], ts(pm, KK[:, 256:288], 0.0, None, A.max))
+        PE(192, ["PM" + H, "Q2", "BLK", "UPI"], [kk], [(KK[:, 288:320], T.Q2[:], pm, True, True), (KK[:, 320:352], T.BLK[:], pm, True, True),
+                                                       (KK[:, 352:384], T.UPI[:], pm, True, True)])
+        SC(64, [kk, "lnw"], ["LN" + H], ac(T.LN[:, h, :], KK[:, 288:352], AF.Ln, bias=T.RF[:, 6:7]))
+        SC(480, ["HA"], ["HWa" + H], ac(HW[:, 32:512], T.HA[:, 32:512], AF.Copy))
+        SC(512, ["HB"], ["HWb" + H], ac(HW[:, 512:1024], T.HB[:, 0:512], AF.Copy))
+        V(64, ["LN" + H], ["XX" + H], ts(T.XX[:, h, :], T.LN[:, h, :], 1.0 / math.log(4.0), 1024.0, A.mult, A.add))
+        V(64, [kk], ["JM" + H], ts(T.JM[:, h, :], KK[:, 352:384], 0.0, None, A.is_gt))
+        PE(128, ["XX" + H, "BL16"], [kk], [(KK[0:32, 384:512], T.XX[:, h, 0:32], T.BL16[:], True, True)])
+        V(128, [kk, "MIM"], ["LT" + H], tt(T.LT[0:32, h, :], KK[0:32, 384:512], T.MIM[0:32, :], A.mult))
+        PE(128, ["LT" + H, "C32", "PCH", "IEH"], [kk], [(KK[:, 128:130], IH, T.PCH[:], True, False), (KK[:, 128:130], T.LT[0:32, h, :], T.C32[0:32, 0:2], False, True)])
+        ji, ju, dj = T.JI[:, h, :], T.JU[:, h, :], T.DJ[:, h, :]
+        V(64, ["NS" + H], ["JI" + H], tt(ji, JJ, SS, A.mult))
+        V(64, ["NS" + H, "UF" + H], ["JU" + H], tt(ju, JJ, T.UF[:, h, :], A.add))
+        V(64, ["JI" + H], ["JI" + H], ts(ji, ji, 5, None, A.arith_shift_right))
+        V(64, ["JI" + H, "JU" + H], ["JU" + H], tt(ju, ji, ju, A.add))
+        V(64, ["JU" + H], ["JU" + H], ts(ju, ju, 4095, None, A.bitwise_and))
+        V(64, ["JU" + H, "NS" + H], ["DJ" + H], tt(dj, ju, JJ, A.subtract))
+        V(64, ["DJ" + H, "JM" + H], ["DJ" + H], tt(dj, dj, T.JM[:, h, :], A.mult))
+        V(64, ["DJ" + H, "S2" + H], ["FCj" + H], tt(T.FC[:, h, 32:64], dj, T.S2[:, h, 1:64:2], A.add))
+        V(64, ["DJ" + H, "NS" + H], ["FOj" + k], tt(FO[:, o + 32:o + 64], dj, JJ, A.add))
+        jg = T.JG[:, h, :]
+        V(64, ["XX" + H, "c1"], ["CDa" + H], ts(T.CD[:, h, 0:32], T.XX[:, h, 32:64], T.RF[:, 4:5], None, A.is_gt))
+        V(64, ["XX" + H, "c2"], ["CDb" + H], ts(T.CD[:, h, 32:64], T.XX[:, h, 0:32], T.RF[:, 5:6], None, A.is_le))
+        V(64, ["CDa" + H, "CDb" + H], ["CD" + H], tt(T.CD[:, h, 64:96], T.CD[:, h, 0:32], T.CD[:, h, 32:64], A.mult))
+        V(64, [kk], ["LS" + H], ts(LS[:], KK[:, 128:130], -32.0 * 1023, None, A.add))
+        V(110, ["LS" + H, "HWz" + H, "HWa" + H, "HWb" + H], ["JG" + H], cp(jg, HW[:].indirect(LS[:])))
+        V(64, ["JG" + H, "S2" + H], ["JG" + H], tt(jg, jg, T.S2[:, h, 0:64:2], A.subtract))
+        V(64, ["JG" + H, "CD" + H], ["JG" + H], tt(jg, jg, T.CD[:, h, 64:96], A.mult))
+        V(64, ["JG" + H, "S2" + H], ["FCs" + H], tt(T.FC[:, h, 0:32], jg, T.S2[:, h, 0:64:2], A.add))
+        V(64, ["JG" + H, "NS" + H], ["FOs" + k], tt(FO[:, o:o + 32], jg, SS, A.add))
+
+    def send(kind, t, h, R):
+        if t == NV - 1:
+            return
+        dst = T.cores[(rank + 3) % 8]
+        rid, pid, _ = topo.addr(dst)
+        n, mask = len(topo.engines(core, dst)), topo.mask(core, dst)
+        o = (2 * t + h) * 64
+        src, out = (T.FO, T.F) if kind == "f" else (T.ZO, T.Z)
+        sem = "ar%s%d%d" % (kind, t + 1, h)
+        add(S, "g", 0.1, R, [("F" if kind == "f" else "Z") + "%d%d" % (t + 1, h)],
+            lambda: g.remote_dma(out[:, o + 128:o + 192], src[:, o:o + 64], T.sem[sem], T.sem.sl, pid, rid, mask), (sem, n), 2.2)
+        S["sends"] += n
+
+    def mining(t, h):
+        k, H = "%d%d" % (t, h), str(h)
+        o = (2 * t + h) * 64
+        MF, E16 = T.MF, T["E16" + H]
+        ef = T.EF[:, h, 0:4]
+        send("f", t, h, ["FOj" + k, "FOs" + k])
+        V(128, ["FCj" + H, "FCs" + H, "SM" + H], ["MF" + H], tt(MF[:, 64 * h:64 * h + 64], T.FC[:, h, :], T.SM[:, h, :], A.mult))
+        kk, bk = BANKS[2 + h], ("MM", "EQ")[h]
+        KK, DD = T[kk], T[bk]
+        PE(128, ["MF" + H, "BLH"], [kk], [(KK[0:64, 384:512], MF[:, 64 * h:64 * h + 64], T.BLH[:], True, True)])
+        V(128, [kk, "MIM"], ["LU" + H], tt(T.LU[0:64, h, :], KK[0:64, 384:512], T.MIM[0:64, :], A.mult))
+        PE(64, ["LU" + H, "C1S"], [kk], [(KK[:, 160:164], T.LU[0:64, h, :], T.C1S[0:64, :], True, True)])
+        V(64, [kk], ["E16" + H], ts(E16[:], KK[:, 160:164], 2048.0, None, A.add))
+        SC(8, [kk], ["EF" + H], ac(ef, KK[:, 160:164], AF.Copy), ac(T.EF[:, h, 4:8], KK[:, 160:164], AF.Copy, bias=2048.0))
+        su = T.SU[:, h, :]
+        V(156, RK + ["E16" + H, "Z5" + H], ["SU" + H], tt(su, T.ROCK[:, 0:4096].indirect(E16[:]), T.Z5[:, h, :], A.add))
+        V(64, ["SU" + H], ["Y1" + H], ts(T.Y1[:, h, :], su, 0.5, None, A.mult))
+        V(64, ["Y1" + H], ["ZO" + k], cp(T.ZO[:, o:o + 64], T.Y1[:, h, :]))
+        send("z", t, h, ["ZO" + k])
+        w = 64 + 64 * h
+        mm = []
+        for c in range(4):
+            mm.append((DD[:, c * w:c * w + w], T.BLH[:], MF[:, 0:w], True, False))
+            mm.append((DD[:, c * w + w - 64:c * w + w], IH, T.MK[:, 256 * t + 64 * c:256 * t + 64 * c + 64], False, True))
+        PE(4 * w + 256, ["MF0", "MF" + H, "MK%d" % t, "BLH", "IEH"], [bk], mm)
+        for c in range(4):
+            du = T.DU[:, h, c * w:c * w + w]
+            V(w, [bk, "EF" + H], ["DU%s%d" % (H, c)], ts(du, DD[:, c * w:c * w + w], T.EF[:, h, c:c + 1], 8192.0, A.is_equal, A.mult))
+            SC(w + 24, ["DU%s%d" % (H, c)], ["DU%s%d" % (H, c), "LO%s%d" % (H, c)], ac(du, du, AF.Copy, accum_out=T.LO[:, 4 * h + c:4 * h + c + 1]))
+        V(64, ["LO%s%d" % (H, c) for c in range(4)] + ["DUMP"], ["OTa" + H], tt(T.OT[:, h, 0:4], T.LO[:, 4 * h:4 * h + 4], T.DUMP[:, 4 * h:4 * h + 4], A.min))
+        V(64, ["OTa" + H, "EF" + H], ["OTb" + H], tt(T.OT[:, h, 4:8], T.OT[:, h, 0:4], T.EF[:, h, 4:8], A.max))
+        V(64, ["OTb" + H], ["OF" + H], cp(T.OF[:, 4 * h:4 * h + 4], T.OT[:, h, 4:8]))
+        V(128, ["SU" + H, "ZZ" + H], ["RR" + H], tt(T.RR[:, h, :], su, T.ZZ[:, h, :], A.subtract))
+        V(64, ["RR" + H], ["RN" + H], ts(T.RN[:, 64 * h:64 * h + 64], T.RR[:, h, :], 1025.5, 0.0, A.add, A.max))
+
+    for t in range(NV):
+        claims(t, 0)
+        if t == 0:
+            claims(t, 1)
+        moves(t, 0)
+        if t > 0:
+            claims(t, 1)
+        moves(t, 1)
+        meetings(t, 0)
+        meetings(t, 1)
+        mining(t, 0)
+        mining(t, 1)
+        V(60 + 128 * 3.8, ["OF0", "OF1", "RN0", "RN1"], RK, cp(T.ROCK[:].indirect(T.OF[:]), T.RN[:]))
+        if t < NV - 1:
+            PE(128, ["JM0", "JM1", "S15"], ["MM"], [(MM[:, 256 + 32 * h:288 + 32 * h], T.S15[:], T.JM[:, h, :], True, True) for h in range(2)])
+            V(64, ["MM"], ["CN"], lambda: v.tensor_reduce(T.CN[:, 0:1], MM[:, 256:320], AxisListType.X, A.add))
+            V(64, ["CN"], ["CI0"], cp(T.CI[:, 0:1], T.CN[:, 0:1]))
+            V(64, ["CI0"], ["CI1"], ts(T.CI[:, 1:2], T.CI[:, 0:1], 3, None, A.bitwise_and))
+            V(64, ["CI1", "LIM"], ["TOP%d" % (t + 1)], ts(T.TOP[:, t + 1:t + 2], T.CI[:, 1:2], T.LIM[:, 0:1], None, A.add))
+    t = NV - 1
+    for h in range(2):
+        o = (2 * t + h) * 64
+        for b in range(2):
+            c = 64 * h + 32 * b
+            SC(32, ["FOj%d%d" % (t, h), "FOs%d%d" % (t, h)], ["YF%d%d" % (h, b)], ac(T.YF[:, c:c + 32], T.FO[:, o + b:o + 64:2], AF.Copy))
+            SC(32, ["ZO%d%d" % (t, h)], ["YZ%d%d" % (h, b)], ac(T.YZ[:, c:c + 32], T.ZO[:, o + b:o + 64:2], AF.Copy))
+    hb = ["00", "01", "10", "11"]
+    add(S, "y", 0.06, ["YF" + x for x in hb], ["oF"], lambda: g.sync.dma_start(T.yf[:], T.YF[:]).then_inc(T.sem.od_f, 16), ("od_f", 16), 2.0)
+    add(S, "y", 0.06, ["YZ" + x for x in hb], ["oZ"], lambda: g.sync.dma_start(T.yz[:], T.YZ[:]).then_inc(T.sem.od_z, 16), ("od_z", 16), 2.0)
+    add(S, "y", 0.06, RK, ["oX"], lambda: g.sync.dma_start(T.yx[:], T.ROCK[:, 0:4096]).then_inc(T.sem.od_x, 16), ("od_x", 16), 5.0)
+    return S
+
+
+def rank_program(g, core, T, topo):
+    if T.rank_of(core) is None:
+        return
+    S = record(g, core, T, topo)
+    order = plan(S)
+    eng = {"v": g.vector, "s": g.scalar, "t": g.tensor, "g": g, "y": g.sync}
+    cnt = issue(S, order, eng, T)
+    for s in sorted(cnt):
+        g.wait_ge(T.sem[s], cnt[s])
+    for s in ("od_f", "od_z", "od_x"):
+        g.wait_ge(T.sem[s], 16)
+    g.wait_ge(T.sem.sl, S["sends"])

@@ -2,7 +2,7 @@ import math
 from concourse.mybir import AluOpType as A, ActivationFunctionType as AF, AxisListType
 
 NV = 5
-NEARV = ((1, 2, 3), (1, 2, 3))
+NEARV = ((0, 1, 2, 3), (0, 1, 2, 3))
 SG = (0,)
 ZXV = (16, 0)
 SCRATCH = {
@@ -13,13 +13,12 @@ SCRATCH = {
     "XR": ("sbuf", [128, 144], "float32"), "T32": ("sbuf", [128, 128], "float32"),
     "BLK": ("sbuf", [128, 128], "bfloat16"), "BLH": ("sbuf", [128, 128], "float16"),
     "R256": ("sbuf", [128, 144], "bfloat16"), "R05": ("sbuf", [128, 144], "bfloat16"), "R1B": ("sbuf", [128, 144], "bfloat16"),
-    "BL16": ("sbuf", [128, 128], "float16"), "MIM": ("sbuf", [128, 128], "float16"), "NI": ("sbuf", [128, 128], "bfloat16"),
-    "C1S": ("sbuf", [128, 4], "float16"), "C32": ("sbuf", [128, 4], "float16"),
-    "LT": ("sbuf", [128, 2, 128], "float16"), "LU": ("sbuf", [128, 2, 128], "float16"),
+    "R1H": ("sbuf", [128, 144], "float16"), "R2H": ("sbuf", [128, 144], "float16"), "NI": ("sbuf", [128, 128], "bfloat16"),
+    "EX": ("sbuf", [128, 1024], "bfloat16"), "EX1": ("sbuf", [128, 512], "bfloat16"), "ZT": ("sbuf", [128, 2, 128], "bfloat16"),
     "XG0": ("sbuf", [128, 1024], "bfloat16"), "XG1": ("sbuf", [128, 1024], "bfloat16"),
     "KM16": ("sbuf", [128, 16], "float32"), "KT": ("sbuf", [128, 16], "float32"),
     "P4": ("sbuf", [128, 16], "float32"), "P4C": ("sbuf", [128, 1], "float32"),
-    "EL": ("sbuf", [128, 16 * 128], "float16"), "PL": ("sbuf", [128, 16 * 128], "bfloat16"),
+    "EL": ("sbuf", [128, 16 * 128], "bfloat16"), "NEG": ("sbuf", [128, 128], "bfloat16"), "PL": ("sbuf", [128, 16 * 128], "bfloat16"),
     "SLB": ("sbuf", [128, 128], "bfloat16"), "Q2": ("sbuf", [128, 128], "bfloat16"),
     "UPI": ("sbuf", [128, 128], "bfloat16"), "S15": ("sbuf", [128, 128], "bfloat16"),
     "ALLC": ("sbuf", [128, 128], "bfloat16"), "K1": ("sbuf", [128, 2, 256], "bfloat16"),
@@ -42,12 +41,12 @@ SCRATCH = {
 for _n, _w, _d in (("UA", 128, "int32"), ("UI", 64, "int32"), ("SI", 64, "int32"), ("QI", 64, "int32"),
                    ("HM", 256, "int32"), ("C4", 256, "int32"), ("DN", 256, "float32"),
                    ("UF", 32, "float32"), ("SM", 64, "float32"), ("ZB", 64, "bfloat16"), ("Z5", 64, "float32"),
-                   ("Z4", 64, "float16"), ("ZZ", 64, "float32"), ("KS", 128, "float32"), ("KM", 128, "float32"),
-                   ("KB", 64, "int32"), ("KC", 64, "int32"), ("PR", 256, "float32"), ("HF", 64, "float16"), ("JC", 32, "float16"),
+                   ("Z4", 64, "bfloat16"), ("KS", 128, "float32"), ("KM", 128, "float32"),
+                   ("KB", 64, "int32"), ("KC", 64, "int32"), ("PR", 256, "float32"), ("HF", 64, "float16"), ("JC", 64, "float16"),
                    ("NS", 64, "float32"), ("S2", 64, "float32"), ("EQB", 512, "bfloat16"),
                    ("PM", 32, "bfloat16"), ("LN", 64, "float32"), ("JM", 32, "bfloat16"), ("XX", 64, "float16"),
                    ("JG", 32, "float32"), ("CD", 96, "bfloat16"), ("JI", 32, "int32"),
-                   ("JU", 32, "int32"), ("DJ", 32, "float32"), ("FC", 64, "float16"),
+                   ("JU", 32, "int32"), ("DJ", 32, "float32"), ("FC", 64, "float32"),
                    ("EF", 8, "float32"), ("SU", 64, "float32"), ("Y1", 64, "int32"), ("RR", 64, "float32"),
                    ("DU", 512, "bfloat16"), ("OT", 8, "float32"), ("D", 4096, "bfloat16"), ("NR", 4096, "bfloat16")):
     SCRATCH[_n] = ("sbuf", [128, 2, _w], _d)
@@ -62,9 +61,15 @@ LOADS = ["wi", "li", "fr", "v0", "v1", "r0", "r1", "r2", "r3"]
 SEMAPHORES = (["sv", "ss", "st", "sg", "sl"] + ["ld_" + n for n in LOADS] + ["od_f", "od_z", "od_x"] +
               ["ar%s%d%d" % (k, t, h) for k in "fz" for t in range(1, NV) for h in range(2)])
 QSEM = {"v": "sv", "s": "ss", "t": "st", "g": "sg"}
-CYC = 0.00083
-PEC = 0.00045
-LAT = 0.08
+ZXP = (1, 1)
+BIAS = {'e1': 0.5, 'm0s': 1.0, 'i0t': -2.5, 'e1t': -5.0, 'c1v': -0.5, 'c0s': -1.0, 'c0t': 13.5, 'm0t': -6.5, 'c0v': -1.0, 'i1t': -6.5,
+        'e1v': -2.0, 'e1s': 4.0, 'e0v': 0.5, 'm1': -2.0, 'c1t': -6.5, 'e0': 0.5, 'i1s': 3.5, 'm1s': -2.0, 'm1v': 0.5, 'c0': 1.0,
+        'e0t': -4.0, 'i0s': -3.5, 'm1t': -1.5, 'e0s': 6.5}
+LOOK = 0.0
+LOV = ((), (1, 3))
+CYC = 0.00104
+PEC = 0.0003
+LAT = 0.15
 SFIX = 78
 
 
@@ -97,7 +102,7 @@ def add(S, q, cost, reads, writes, fn, sig=None, lat=0.0):
     for k in reads:
         if k not in BANKS and k not in writes:
             S["r"].setdefault(k, []).append(i)
-    S["ops"].append({"q": q, "cost": cost, "deps": deps, "fn": fn, "sig": sig, "lat": lat, "nm": " ".join(writes)})
+    S["ops"].append({"q": q, "cost": cost, "deps": deps, "fn": fn, "sig": sig, "lat": lat, "st": S.get("st", ""), "nm": " ".join(writes)})
     return i
 
 
@@ -115,6 +120,7 @@ def plan(S):
         for k in succ[i]:
             b = max(b, pri[k] + (o["lat"] if o["sig"] else (LAT if ops[k]["deps"][i] else 0.0)))
         pri[i] = b + o["cost"]
+    pri = [p + BIAS.get(o["st"], 0.0) + BIAS.get(o["st"] + o["q"], 0.0) for p, o in zip(pri, ops)]
     left = [len(o["deps"]) for o in ops]
     ready = {}
     est = [0.0] * n
@@ -135,7 +141,7 @@ def plan(S):
         lst = ready[q]
         c = max((i for i in lst if est[i] <= st + 1e-9), key=lambda i: (pri[i], -i))
         for i in lst:
-            if pri[i] > pri[c] and est[i] < st + 0.5 * ops[c]["cost"]:
+            if pri[i] > pri[c] and est[i] < st + LOOK * ops[c]["cost"]:
                 c = i
         st = max(st, est[c])
         lst.remove(c)
@@ -277,22 +283,25 @@ def record(g, core, T, topo):
     V(64, ["PIs"], ["PIt"], ts(T.PI[:, 4:5], T.PI[:, 3:4], 15, None, A.bitwise_and))
     V(64, ["PIt"], ["rp1"], cp(T.RF[:, 3:4], T.PI[:, 4:5]))
     V(64, [], ["q25"], ms(T.RF[:, 6:7], 0.25))
-    V(64, ["BLH"], ["BL16"], ts(T.BL16[:], T.BLH[:], 0.0625, None, A.mult))
-    V(128, ["CR", "r"], ["MIM"], ts(T.MIM[:], T.CR[:], r, None, A.is_equal))
-    V(64, ["KM0", "gp"], ["C1S"], ts(T.C1S[:], T.KM16[:, 0:4], gp, None, A.is_equal))
-    V(64, ["C1S"], ["C32"], ts(T.C32[:], T.C1S[:], 32.0, None, A.mult))
+    V(64, [], ["b129"], ms(T.RF[:, 8:9], 129.5))
     V(64, ["IEB"], ["NI"], ts(T.NI[:], T.IEB[:, 15:143], -1.0, None, A.mult))
-    for n, c in (("R256", 256.0), ("R05", 0.5), ("R1B", 1.0)):
+    for n, c in (("R256", 256.0), ("R05", 0.5), ("R1B", 1.0), ("R1H", 1.0), ("R2H", 2.0)):
         V(143, ["XR", "gp16"], [n], ts(T[n][:, 0:143], T.XR[:, 0:143], T.RF[:, 2:3], c, A.is_equal, A.mult))
     V(64, [], ["ALLC"], ms(T.ALLC[:], 1.0 / 128))
-    V(512, [], ["K1"], *[ms(T.K1[:, h, 64 * m:64 * m + 64], 64.0 * m + (23 if m in NEARV[h] else 31)) for m in range(4) for h in range(2)])
+    for h in range(2):
+        for m in range(4):
+            G(0.28, ["ONES"], ["K1%d%d" % (h, m)], (lambda h, m: lambda: g.affine_select(T.K1[:, h, 64 * m:64 * m + 64], T.ONES[:, 0:64], [[0, 64]], A.is_gt, 64.0 * m + (23 if m in NEARV[h] else 31), 0, 0))(h, m))
     V(80, ["IEB"], ["IEH"], cp(T.IEH[:, 0:158], T.IEB[:, 0:158]))
     V(128, ["IEB"], ["I32"], cp(T.I32[:], T.IEB[:, 15:143]))
     V(64, ["KM0", "r"], ["KT"], ts(T.KT[:], T.KM16[:], r, None, A.is_equal))
-    V(64, ["KT"], ["KM0"], ts(T.KM16[:], T.KT[:], -1.0, None, A.mult))
-    V(16 * 64, ["BLK", "KM0"], ["EL"], *[ts(T.EL[:, 128 * l:128 * l + 128], T.BLK[:], T.KM16[:, l:l + 1], None, A.mult) for l in range(16)])
-    V(16 * 64, [], ["P4"], *[ms(T.P4[:, l:l + 1], 4.0 ** l) for l in range(16)])
-    V(64, ["P4", "KT"], ["P4b"], tt(T.P4[:], T.P4[:], T.KT[:], A.mult))
+    V(512, [], ["W1"], ms(T.EX1[:], 1.0))
+    for b in range(2):
+        G(1.05, ["W1"], ["EX%d" % b], (lambda b: lambda: g.affine_select(T.EX[:, 512 * b:512 * b + 512], T.EX1[:], [[-1, 32], [0, 16]], A.is_equal, 0.0, -32 * b, 1))(b))
+    V(64, [], ["NEG"], ms(T.NEG[:], -1.0))
+    for l in range(16):
+        G(0.4, ["NEG"], ["EL%d" % l], (lambda l: lambda: g.affine_select(T.EL[:, 128 * l:128 * l + 128], T.NEG[:], [[-16, 8], [0, 16]], A.is_equal, 0.0, -l, 1))(l))
+        G(0.18, ["q25"], ["P4%d" % l], (lambda l: lambda: g.affine_select(T.P4[:, l:l + 1], T.RF[:, 6:7], [[0, 1]], A.is_gt, 4.0 ** l, 0, 0))(l))
+    V(64, ["P4%d" % l for l in range(16)] + ["KT"], ["P4b"], tt(T.P4[:], T.P4[:], T.KT[:], A.mult))
     V(64, ["P4b"], ["P4C"], lambda: v.tensor_reduce(T.P4C[:], T.P4[:], AxisListType.X, A.add))
     V(64, ["BLK", "P4C"], ["Q2"], ts(T.Q2[:], T.BLK[:], T.P4C[:, 0:1], None, A.mult))
     V(128, ["CR", "r"], ["T32"], ts(T.T32[:], T.CR[:], r, -(2.0 ** 40), A.is_gt, A.mult))
@@ -340,21 +349,28 @@ def record(g, core, T, topo):
         V(256, [xk, "UAh" + H], ["HM" + H], *[tt(T.HM[:, h, 64 * m:64 * m + 64], X[:, 128 + 64 * m:192 + 64 * m], hh, A.add) for m in range(4)])
         V(256, ["HM" + H], ["C4" + H], *[ts(T.C4[:, h, 64 * m:64 * m + 64], T.HM[:, h, 64 * m:64 * m + 64], 4 + m, 4095, A.arith_shift_right, A.bitwise_and) for m in range(4)])
         V(256, ["C4" + H], ["CO" + H], cp(CO[:], T.C4[:, h, :]))
-        for b in range(0, 16, 4):
-            if b < ZXV[h]:
-                V(256, ["Z" + k], ["ZX%s%d" % (H, b)], *[cp(ZX[:, p:1024:16], Z) for p in range(b, b + 4)])
-            else:
-                SC(256, ["Z" + k], ["ZX%s%d" % (H, b)], *[ac(ZX[:, p:1024:16], Z, AF.Copy) for p in range(b, b + 4)])
+        if ZXP[h]:
+            PE(128, ["Z" + k, "IEB"], ["HA"], [(T.HA[0:64, 0:128], Z, T.IEB[:, 15:143], True, True)])
+            SC(128, ["HA"], ["ZT" + H], ac(T.ZT[0:64, h, :], T.HA[0:64, 0:128], AF.Copy))
+            for b, bk in ((0, "HB"), (1, "HA")):
+                PE(512, ["ZT" + H, "EX0", "EX1"], [bk], [(T[bk][:], T.ZT[0:64, h, :], T.EX[0:64, 512 * b:512 * b + 512], True, True)])
+                SC(512, [bk], ["ZX%s%d" % (H, 8 * b), "ZX%s%d" % (H, 8 * b + 4)], ac(ZX[:, 512 * b:512 * b + 512], T[bk][:], AF.Copy))
+        else:
+            for b in range(0, 16, 4):
+                if b < ZXV[h]:
+                    V(256, ["Z" + k], ["ZX%s%d" % (H, b)], *[cp(ZX[:, p:1024:16], Z) for p in range(b, b + 4)])
+                else:
+                    SC(256, ["Z" + k], ["ZX%s%d" % (H, b)], *[ac(ZX[:, p:1024:16], Z, AF.Copy) for p in range(b, b + 4)])
         V(64, ["UA" + H], ["SI" + H], ts(T.SI[:, h, :], T.UA[:, h, 64:128], 15, None, A.bitwise_and))
         V(256, [xk, "C4" + H], ["DN" + H], *[tt(T.DN[:, h, 64 * m:64 * m + 64], T.C4[:, h, 64 * m:64 * m + 64], nX, A.subtract) for m in range(4)])
-        PE(256, ["F" + k, "I32"], [xk], [(X[:, 448:512], T.I32[:], F, True, False)])
         V(64, ["UI" + H], ["UF" + H], ts(T.UF[:, h, :], T.UI[:, h, 1:64:2], -1.0, 0.5, A.add, A.mult))
         V(128, ["SI" + H, "rp1"], ["SM" + H], *[ts(T.SM[:, h, 32 * b:32 * b + 32], T.SI[:, h, b:64:2], T.RF[:, 3:4], None, A.is_equal) for b in range(2)])
         zb = T.ZB[:, h, :]
         SC(64, ["Z" + k], ["ZB" + H], *[ac(T.ZB[:, h, 32 * b:32 * b + 32], T.Z[:, o + b:o + 64:2], AF.Copy) for b in range(2)])
         SC(64, ["ZB" + H], ["Z5" + H], ac(T.Z5[:, h, :], zb, AF.Copy, bias=-0.5))
-        V(64, ["ZB" + H], ["Z4" + H], ts(T.Z4[:, h, :], zb, 0.25, 1025 - 0.375, A.mult, A.add))
-        V(128, ["ZB" + H, "Z4" + H], ["ZZ" + H], tt(T.ZZ[:, h, :], T.Z4[:, h, :], zb, A.add))
+        SC(64, ["ZB" + H], ["Z4" + H], ac(T.Z4[:, h, :], zb, AF.Copy, scale=0.25, bias=129 - 0.375))
+        PE(128, ["ZB" + H, "Z4" + H, "IEB"], [xk], [(X[:, 0:64], T.IEB[:, 15:143], T.Z4[:, h, :], True, False), (X[:, 0:64], T.IEB[:, 15:143], zb, False, True)])
+        PE(256, ["F" + k, "I32"], [xk], [(X[:, 448:512], T.I32[:], F, True, False)])
 
     def moves(t, h):
         k, H = "%d%d" % (t, h), str(h)
@@ -362,7 +378,6 @@ def record(g, core, T, topo):
         KK = T[kk]
         CO, ZX = T["CO" + H], T["ZX" + H]
         o = (2 * t + h) * 64
-        PE(256, ["ALLC", "K1"], [kk], [(KK[:, 0:256], T.ALLC[:], T.K1[:, h, :], True, False)])
         for m in range(4):
             d, n = "D%d%d" % (h, m), "N%d%d" % (h, m)
             dm, nm = T.D[:, h, 1024 * m:1024 * m + 1024], T.NR[:, h, 1024 * m:1024 * m + 1024]
@@ -385,11 +400,14 @@ def record(g, core, T, topo):
 
         def keys(m, near):
             w, src, b = (("R1B" if m in NEARV[h] else "R05"), T.NR, "N") if near else ("R256", T.D, "D")
-            PE(1024, ["%s%d%d%s" % (b, h, m, x) for x in "ab"] + [w], [kk], [(KK[:, 64 * m:64 * m + 64], T[w][:, 15 - p:143 - p], src[:, h, 1024 * m + p:1024 * m + 1024:16], False, near and m == 3 and p == 15) for p in range(16)])
-        for m, near in ((0, 0), (1, 0), (0, 1), (2, 0), (1, 1), (3, 0), (2, 1), (3, 1)):
-            keys(m, bool(near))
-        V(128, [kk], ["KS" + H], cp(T.KS[:, h, :], KK[:, 128:256]))
-        V(128, [kk, "KS" + H], ["KM" + H], tt(T.KM[:, h, :], KK[:, 0:128], T.KS[:, h, :], A.min))
+            PE(1024, ["%s%d%d%s" % (b, h, m, x) for x in "ab"] + [w], [kk], [(KK[:, 64 * m:64 * m + 64], T[w][:, 15 - p:143 - p], src[:, h, 1024 * m + p:1024 * m + 1024:16], False, near and m % 2 == 1 and p == 15) for p in range(16)])
+        for b in (0, 1):
+            PE(128, ["ALLC"] + ["K1%d%d" % (h, m) for m in range(4)], [kk], [(KK[:, 128 * b:128 * b + 128], T.ALLC[:], T.K1[:, h, 128 * b:128 * b + 128], True, False)])
+            for m, near in ((0, 0), (1, 0), (0, 1), (1, 1)):
+                keys(2 * b + m, bool(near))
+            if b == 0:
+                SC(128, [kk], ["KS" + H], ac(T.KS[:, h, :], KK[:, 0:128], AF.Copy))
+        V(128, [kk, "KS" + H], ["KM" + H], tt(T.KM[:, h, :], KK[:, 128:256], T.KS[:, h, :], A.min))
         V(128, ["KM" + H], ["KB" + H], tt(T.KB[:, h, :], T.KM[:, h, 0:64], T.KM[:, h, 64:128], A.min))
         V(64, ["KB" + H], ["KC" + H], ts(T.KC[:, h, :], T.KB[:, h, :], 255, 5, A.bitwise_and, A.arith_shift_right))
         V(256, ["KC" + H], [kk], *[ts(KK[:, 256 + 64 * m:320 + 64 * m], T.KC[:, h, :], float(2 * m + 1), None, A.is_equal) for m in range(4)])
@@ -405,7 +423,8 @@ def record(g, core, T, topo):
         HW, LS, FO = T["HW" + H], T["LS" + H], T.FO
         SS, JJ = T.NS[:, h, 0:64:2], T.NS[:, h, 1:64:2]
         V(64, [xk], ["HF" + H], ts(T.HF[:, h, :], NP, 0.125, 1025 - 0.4375, A.mult, A.add))
-        V(64, [xk], ["JC" + H], ts(T.JC[:, h, :], T[xk][:, 449:512:2], -2048.0, None, A.add))
+        V(64, [xk], ["JC" + H], ts(T.JC[:, h, 0:32], T[xk][:, 449:512:2], -2048.0, None, A.add))
+        V(64, [xk], ["JS" + H], ts(T.JC[:, h, 32:64], T[xk][:, 448:512:2], -1.0, 2048.0, A.mult, A.add))
         SC(64, [xk], ["NS" + H], ac(T.NS[:, h, :], NP, AF.Copy))
         SC(64, ["NS" + H], ["S2" + H], ac(T.S2[:, h, :], T.NS[:, h, :], AF.Copy, bias=-2048.0))
         for b, bk in ((0, "EQ"), (1, "MM")):
@@ -414,12 +433,16 @@ def record(g, core, T, topo):
                 dd = T[bk][:, 32 * l:32 * l + 32]
                 mm.append((dd, IH, T.HF[:, h, 1:64:2], True, False))
                 mm.append((dd, T.EL[:, 128 * (8 * b + l):128 * (8 * b + l) + 128], T.HF[:, h, 0:64:2], False, True))
-            PE(16 * 64, ["HF" + H, "EL", "IEH"], [bk], mm)
+            PE(16 * 64, ["HF" + H, "IEH"] + ["EL%d" % l for l in range(16)], [bk], mm)
             V(256, [bk], ["EQB%s%d" % (H, b)], ts(T.EQB[:, h, 256 * b:256 * b + 256], T[bk][:, 0:256], 0.0, None, A.is_equal))
             PE(512, ["EQB%s%d" % (H, b)] + PLK, [kk], [(KK[:, 256:288], T.PL[:, 128 * l:128 * l + 128], T.EQB[:, h, 32 * l:32 * l + 32], l == 0, l == 15) for l in range(8 * b, 8 * b + 8)])
-        jc, pm = T.JC[:, h, :], T.PM[:, h, :]
-        PE(15 * 64, ["JC" + H, "IEH"], ["HA"], [(T.HA[:, 32 * s:32 * s + 32], T.IEH[:, s - 1:s + 127], jc, True, True) for s in range(1, 16)])
-        PE(16 * 64, ["JC" + H, "IEH"], ["HB"], [(T.HB[:, 32 * s - 512:32 * s - 480], T.IEH[:, s - 1:s + 127], jc, True, True) for s in range(16, 32)])
+        pm = T.PM[:, h, :]
+        for bk, s0, s1 in [("HA" if x < 16 else "HB", max(x, 1), x + 4) for x in range(0, 32, 4)]:
+            mm = []
+            for s in range(s0, s1):
+                dd = T[bk][:, 32 * (s % 16):32 * (s % 16) + 32]
+                mm += [(dd, T.IEH[:, s - 1:s + 127], T.JC[:, h, 0:32], True, False), (dd, IH, T.JC[:, h, 32:64], False, True)]
+            PE(64 * len(mm), ["JC" + H, "JS" + H, "IEH"], [bk], mm)
         V(64, [kk], ["PM" + H], ts(pm, KK[:, 256:288], 0.0, None, A.max))
         PE(192, ["PM" + H, "Q2", "BLK", "UPI"], [kk], [(KK[:, 288:320], T.Q2[:], pm, True, True), (KK[:, 320:352], T.BLK[:], pm, True, True),
                                                        (KK[:, 352:384], T.UPI[:], pm, True, True)])
@@ -428,9 +451,8 @@ def record(g, core, T, topo):
         SC(512, ["HB"], ["HWb" + H], ac(HW[:, 512:1024], T.HB[:, 0:512], AF.Copy))
         V(64, ["LN" + H], ["XX" + H], ts(T.XX[:, h, :], T.LN[:, h, :], 1.0 / math.log(4.0), 1024.0, A.mult, A.add))
         V(64, [kk], ["JM" + H], ts(T.JM[:, h, :], KK[:, 352:384], 0.0, None, A.is_gt))
-        PE(128, ["XX" + H, "BL16"], [kk], [(KK[0:32, 384:512], T.XX[:, h, 0:32], T.BL16[:], True, True)])
-        V(128, [kk, "MIM"], ["LT" + H], tt(T.LT[0:32, h, :], KK[0:32, 384:512], T.MIM[0:32, :], A.mult))
-        PE(128, ["LT" + H, "C32", "PCH", "IEH"], [kk], [(KK[:, 128:130], IH, T.PCH[:], True, False), (KK[:, 128:130], T.LT[0:32, h, :], T.C32[0:32, 0:2], False, True)])
+        PE(17 * 64, ["XX" + H, "R2H", "PCH", "IEH"], [kk], [(KK[:, 128:130], IH, T.PCH[:], True, False)] +
+           [(KK[:, 128:130], T.R2H[:, 15 - p:143 - p], T.XX[:, h, p:32:16], False, p == 15) for p in range(16)])
         ji, ju, dj = T.JI[:, h, :], T.JU[:, h, :], T.DJ[:, h, :]
         V(64, ["NS" + H], ["JI" + H], tt(ji, JJ, SS, A.mult))
         V(64, ["NS" + H, "UF" + H], ["JU" + H], tt(ju, JJ, T.UF[:, h, :], A.add))
@@ -440,17 +462,15 @@ def record(g, core, T, topo):
         V(64, ["JU" + H, "NS" + H], ["DJ" + H], tt(dj, ju, JJ, A.subtract))
         V(64, ["DJ" + H, "JM" + H], ["DJ" + H], tt(dj, dj, T.JM[:, h, :], A.mult))
         V(64, ["DJ" + H, "S2" + H], ["FCj" + H], tt(T.FC[:, h, 32:64], dj, T.S2[:, h, 1:64:2], A.add))
-        V(64, ["DJ" + H, "NS" + H], ["FOj" + k], tt(FO[:, o + 32:o + 64], dj, JJ, A.add))
+        SC(32, ["FCj" + H], ["FOj" + k], ac(FO[:, o + 32:o + 64], T.FC[:, h, 32:64], AF.Copy, bias=2048.0))
         jg = T.JG[:, h, :]
         V(64, ["XX" + H, "c1"], ["CDa" + H], ts(T.CD[:, h, 0:32], T.XX[:, h, 32:64], T.RF[:, 4:5], None, A.is_gt))
         V(64, ["XX" + H, "c2"], ["CDb" + H], ts(T.CD[:, h, 32:64], T.XX[:, h, 0:32], T.RF[:, 5:6], None, A.is_le))
         V(64, ["CDa" + H, "CDb" + H], ["CD" + H], tt(T.CD[:, h, 64:96], T.CD[:, h, 0:32], T.CD[:, h, 32:64], A.mult))
         V(64, [kk], ["LS" + H], ts(LS[:], KK[:, 128:130], -32.0 * 1023, None, A.add))
-        V(110, ["LS" + H, "HWz" + H, "HWa" + H, "HWb" + H], ["JG" + H], cp(jg, HW[:].indirect(LS[:])))
-        V(64, ["JG" + H, "S2" + H], ["JG" + H], tt(jg, jg, T.S2[:, h, 0:64:2], A.subtract))
-        V(64, ["JG" + H, "CD" + H], ["JG" + H], tt(jg, jg, T.CD[:, h, 64:96], A.mult))
+        V(110, ["LS" + H, "CD" + H, "HWz" + H, "HWa" + H, "HWb" + H], ["JG" + H], tt(jg, HW[:].indirect(LS[:]), T.CD[:, h, 64:96], A.mult))
         V(64, ["JG" + H, "S2" + H], ["FCs" + H], tt(T.FC[:, h, 0:32], jg, T.S2[:, h, 0:64:2], A.add))
-        V(64, ["JG" + H, "NS" + H], ["FOs" + k], tt(FO[:, o:o + 32], jg, SS, A.add))
+        SC(32, ["FCs" + H], ["FOs" + k], ac(FO[:, o:o + 32], T.FC[:, h, 0:32], AF.Copy, bias=2048.0))
 
     def send(kind, t, h, R):
         if t == NV - 1:
@@ -474,11 +494,10 @@ def record(g, core, T, topo):
         V(128, ["FCj" + H, "FCs" + H, "SM" + H], ["MF" + H], tt(MF[:, 64 * h:64 * h + 64], T.FC[:, h, :], T.SM[:, h, :], A.mult))
         kk, bk = BANKS[2 + h], ("MM", "EQ")[h]
         KK, DD = T[kk], T[bk]
-        PE(128, ["MF" + H, "BLH"], [kk], [(KK[0:64, 384:512], MF[:, 64 * h:64 * h + 64], T.BLH[:], True, True)])
-        V(128, [kk, "MIM"], ["LU" + H], tt(T.LU[0:64, h, :], KK[0:64, 384:512], T.MIM[0:64, :], A.mult))
-        PE(64, ["LU" + H, "C1S"], [kk], [(KK[:, 160:164], T.LU[0:64, h, :], T.C1S[0:64, :], True, True)])
+        PE(1024, ["MF" + H, "R1H"], [kk], [(KK[:, 160:164], T.R1H[:, 15 - p:143 - p], MF[:, 64 * h + p:64 * h + 64:16], p == 0, p == 15) for p in range(16)])
         V(64, [kk], ["E16" + H], ts(E16[:], KK[:, 160:164], 2048.0, None, A.add))
-        SC(8, [kk], ["EF" + H], ac(ef, KK[:, 160:164], AF.Copy), ac(T.EF[:, h, 4:8], KK[:, 160:164], AF.Copy, bias=2048.0))
+        V(64, [kk], ["EF" + H], cp(ef, KK[:, 160:164]))
+        SC(4, [kk], ["EG" + H], ac(T.EF[:, h, 4:8], KK[:, 160:164], AF.Copy, bias=2048.0))
         su = T.SU[:, h, :]
         V(156, RK + ["E16" + H, "Z5" + H], ["SU" + H], tt(su, T.ROCK[:, 0:4096].indirect(E16[:]), T.Z5[:, h, :], A.add))
         V(64, ["SU" + H], ["Y1" + H], ts(T.Y1[:, h, :], su, 0.5, None, A.mult))
@@ -493,26 +512,36 @@ def record(g, core, T, topo):
         for c in range(4):
             du = T.DU[:, h, c * w:c * w + w]
             V(w, [bk, "EF" + H], ["DU%s%d" % (H, c)], ts(du, DD[:, c * w:c * w + w], T.EF[:, h, c:c + 1], 8192.0, A.is_equal, A.mult))
-            SC(w + 24, ["DU%s%d" % (H, c)], ["DU%s%d" % (H, c), "LO%s%d" % (H, c)], ac(du, du, AF.Copy, accum_out=T.LO[:, 4 * h + c:4 * h + c + 1]))
-        V(64, ["LO%s%d" % (H, c) for c in range(4)] + ["DUMP"], ["OTa" + H], tt(T.OT[:, h, 0:4], T.LO[:, 4 * h:4 * h + 4], T.DUMP[:, 4 * h:4 * h + 4], A.min))
-        V(64, ["OTa" + H, "EF" + H], ["OTb" + H], tt(T.OT[:, h, 4:8], T.OT[:, h, 0:4], T.EF[:, h, 4:8], A.max))
-        V(64, ["OTb" + H], ["OF" + H], cp(T.OF[:, 4 * h:4 * h + 4], T.OT[:, h, 4:8]))
-        V(128, ["SU" + H, "ZZ" + H], ["RR" + H], tt(T.RR[:, h, :], su, T.ZZ[:, h, :], A.subtract))
-        V(64, ["RR" + H], ["RN" + H], ts(T.RN[:, 64 * h:64 * h + 64], T.RR[:, h, :], 1025.5, 0.0, A.add, A.max))
+            j = 4 * h + c
+            lo = T.LO[:, j:j + 1]
+            if c in LOV[h]:
+                V(w, ["DU%s%d" % (H, c)], ["LO%s%d" % (H, c)], (lambda lo, du: lambda: v.tensor_reduce(lo, du, AxisListType.X, A.add))(lo, du))
+            else:
+                SC(w + 24, ["DU%s%d" % (H, c)], ["DU%s%d" % (H, c), "LO%s%d" % (H, c)], ac(du, du, AF.Copy, accum_out=lo))
+            V(64, ["LO%s%d" % (H, c), "DUMP", "EG" + H], ["OF%d" % j], ts(T.OF[:, j:j + 1], lo, T.DUMP[:, j:j + 1], T.EF[:, h, 4 + c:5 + c], A.min, A.max))
+        V(64, ["SU" + H, "X" + H], ["RR" + H], tt(T.RR[:, h, :], su, T["X" + H][:, 0:64], A.subtract))
+        SC(64, ["RR" + H, "b129"], ["RN" + H], ac(T.RN[:, 64 * h:64 * h + 64], T.RR[:, h, :], AF.Relu, bias=T.RF[:, 8:9]))
+
+    names = [(claims, "c"), (moves, "m"), (meetings, "e"), (mining, "i")]
+
+    def stage(f, t, h):
+        S["st"] = [n for f2, n in names if f2 == f][0] + str(h)
+        f(t, h)
+        S["st"] = ""
 
     for t in range(NV):
-        claims(t, 0)
+        stage(claims, t, 0)
         if t == 0:
-            claims(t, 1)
-        moves(t, 0)
+            stage(claims, t, 1)
+        stage(moves, t, 0)
         if t > 0:
-            claims(t, 1)
-        moves(t, 1)
-        meetings(t, 0)
-        meetings(t, 1)
-        mining(t, 0)
-        mining(t, 1)
-        V(60 + 128 * 3.8, ["OF0", "OF1", "RN0", "RN1"], RK, cp(T.ROCK[:].indirect(T.OF[:]), T.RN[:]))
+            stage(claims, t, 1)
+        stage(moves, t, 1)
+        stage(meetings, t, 0)
+        stage(meetings, t, 1)
+        stage(mining, t, 0)
+        stage(mining, t, 1)
+        V(60 + 128 * 3.8, ["OF%d" % j for j in range(8)] + ["RN0", "RN1"], RK, cp(T.ROCK[:].indirect(T.OF[:]), T.RN[:]))
         if t < NV - 1:
             PE(128, ["JM0", "JM1", "S15"], ["MM"], [(MM[:, 256 + 32 * h:288 + 32 * h], T.S15[:], T.JM[:, h, :], True, True) for h in range(2)])
             V(64, ["MM"], ["CN"], lambda: v.tensor_reduce(T.CN[:, 0:1], MM[:, 256:320], AxisListType.X, A.add))

import math
from concourse.mybir import AluOpType as A, ActivationFunctionType as AF, AxisListType

NV = 5
NEARV = ((0, 1, 2, 3), (0, 1, 2, 3))
SG = (0,)
ZXV = (16, 0)
SCRATCH = {
    "PI": ("sbuf", [128, 8], "int32"), "RF": ("sbuf", [128, 16], "float32"),
    "ONES": ("sbuf", [128, 160], "bfloat16"), "IEB": ("sbuf", [128, 160], "bfloat16"),
    "IEH": ("sbuf", [128, 160], "float16"), "I32": ("sbuf", [128, 128], "float32"),
    "GR": ("sbuf", [128, 128], "float32"), "CR": ("sbuf", [128, 128], "float32"),
    "XR": ("sbuf", [128, 144], "float32"), "T32": ("sbuf", [128, 128], "float32"),
    "BLK": ("sbuf", [128, 128], "bfloat16"), "BLH": ("sbuf", [128, 128], "float16"),
    "R256": ("sbuf", [128, 144], "bfloat16"), "R05": ("sbuf", [128, 144], "bfloat16"), "R1B": ("sbuf", [128, 144], "bfloat16"),
    "R1H": ("sbuf", [128, 144], "float16"), "R2H": ("sbuf", [128, 144], "float16"), "NI": ("sbuf", [128, 128], "bfloat16"),
    "EX": ("sbuf", [128, 1024], "bfloat16"), "EX1": ("sbuf", [128, 512], "bfloat16"), "ZT": ("sbuf", [128, 2, 128], "bfloat16"),
    "XG0": ("sbuf", [128, 1024], "bfloat16"), "XG1": ("sbuf", [128, 1024], "bfloat16"),
    "KM16": ("sbuf", [128, 16], "float32"), "KT": ("sbuf", [128, 16], "float32"),
    "P4": ("sbuf", [128, 16], "float32"), "P4C": ("sbuf", [128, 1], "float32"),
    "EL": ("sbuf", [128, 16 * 128], "bfloat16"), "NEG": ("sbuf", [128, 128], "bfloat16"), "PL": ("sbuf", [128, 16 * 128], "bfloat16"),
    "SLB": ("sbuf", [128, 128], "bfloat16"), "Q2": ("sbuf", [128, 128], "bfloat16"),
    "UPI": ("sbuf", [128, 128], "bfloat16"), "S15": ("sbuf", [128, 128], "bfloat16"),
    "ALLC": ("sbuf", [128, 128], "bfloat16"), "K1": ("sbuf", [128, 2, 256], "bfloat16"),
    "BB": ("sbuf", [128, 4], "float32"), "PCH": ("sbuf", [128, 2], "float16"),
    "DUMP": ("sbuf", [128, 8], "float32"), "MK": ("sbuf", [128, 5 * 256], "float16"),
    "PRW": ("sbuf", [128, 5 * 64], "float32"), "JCI": ("sbuf", [128, 16], "int32"),
    "PCI": ("sbuf", [128, 5 * 4], "int32"), "PTI": ("sbuf", [128, 5 * 4], "int32"),
    "PCF": ("sbuf", [128, 5 * 4], "float32"),
    "W2": ("sbuf", [128, 128], "bfloat16"), "WI": ("sbuf", [128, 2], "int32"),
    "WF": ("sbuf", [128, 2], "float32"), "LIM": ("sbuf", [128, 1], "float32"),
    "TOP": ("sbuf", [128, 8], "float32"), "CN": ("sbuf", [128, 4], "float32"), "CI": ("sbuf", [128, 4], "int32"),
    "FI": ("sbuf", [128, 128], "int32"),
    "F": ("sbuf", [128, NV * 128], "float32"), "FO": ("sbuf", [128, NV * 128], "float32"),
    "Z": ("sbuf", [128, NV * 128], "bfloat16"), "ZO": ("sbuf", [128, NV * 128], "bfloat16"),
    "ROCK": ("sbuf", [128, 4096 + 128], "bfloat16"),
    "YF": ("sbuf", [128, 128], "float32"), "YZ": ("sbuf", [128, 128], "bfloat16"),
    "MF": ("sbuf", [128, 128], "float16"), "RN": ("sbuf", [128, 128], "bfloat16"),
    "OF": ("sbuf", [128, 8], "uint16"), "LO": ("sbuf", [128, 8], "float32"),
}
for _n, _w, _d in (("UA", 128, "int32"), ("UI", 64, "int32"), ("SI", 64, "int32"), ("QI", 64, "int32"),
                   ("HM", 256, "int32"), ("C4", 256, "int32"), ("DN", 256, "float32"),
                   ("UF", 32, "float32"), ("SM", 64, "float32"), ("ZB", 64, "bfloat16"), ("Z5", 64, "float32"),
                   ("Z4", 64, "bfloat16"), ("KS", 128, "float32"), ("KM", 128, "float32"),
                   ("KB", 64, "int32"), ("KC", 64, "int32"), ("PR", 256, "float32"), ("HF", 64, "float16"), ("JC", 64, "float16"),
                   ("NS", 64, "float32"), ("S2", 64, "float32"), ("EQB", 512, "bfloat16"),
                   ("PM", 32, "bfloat16"), ("LN", 64, "float32"), ("JM", 32, "bfloat16"), ("XX", 64, "float16"),
                   ("JG", 32, "float32"), ("CD", 96, "bfloat16"), ("JI", 32, "int32"),
                   ("JU", 32, "int32"), ("DJ", 32, "float32"), ("FC", 64, "float32"),
                   ("EF", 8, "float32"), ("SU", 64, "float32"), ("Y1", 64, "int32"), ("RR", 64, "float32"),
                   ("DU", 512, "bfloat16"), ("OT", 8, "float32"), ("D", 4096, "bfloat16"), ("NR", 4096, "bfloat16")):
    SCRATCH[_n] = ("sbuf", [128, 2, _w], _d)
for _h in "01":
    for _n, _w, _d in (("CO", 256, "uint16"), ("ZX", 1024, "bfloat16"), ("HW", 1024, "float32"), ("LS", 2, "uint16"), ("E16", 4, "uint16")):
        SCRATCH[_n + _h] = ("sbuf", [128, _w], _d)
BANKS = ["X0", "X1", "K0", "K1b", "EQ", "HA", "HB", "MM"]
for _n in BANKS:
    SCRATCH[_n] = ("psum", [128, 512], "float32")

LOADS = ["wi", "li", "fr", "v0", "v1", "r0", "r1", "r2", "r3"]
SEMAPHORES = (["sv", "ss", "st", "sg", "sl"] + ["ld_" + n for n in LOADS] + ["od_f", "od_z", "od_x"] +
              ["ar%s%d%d" % (k, t, h) for k in "fz" for t in range(1, NV) for h in range(2)])
QSEM = {"v": "sv", "s": "ss", "t": "st", "g": "sg"}
ZXP = (1, 1)
BIAS = {'e1': 0.5, 'm0s': 1.0, 'i0t': -2.5, 'e1t': -5.0, 'c1v': -0.5, 'c0s': -1.0, 'c0t': 13.5, 'm0t': -6.5, 'c0v': -1.0, 'i1t': -6.5,
        'e1v': -2.0, 'e1s': 4.0, 'e0v': 0.5, 'm1': -2.0, 'c1t': -6.5, 'e0': 0.5, 'i1s': 3.5, 'm1s': -2.0, 'm1v': 0.5, 'c0': 1.0,
        'e0t': -4.0, 'i0s': -3.5, 'm1t': -1.5, 'e0s': 6.5}
LOOK = 0.0
LOV = ((), (1, 3))
CYC = 0.00104
PEC = 0.0003
LAT = 0.15
SFIX = 78


def add(S, q, cost, reads, writes, fn, sig=None, lat=0.0):
    i = len(S["ops"])
    deps = {}

    def dep(j, sem):
        if j != i:
            deps[j] = deps.get(j, False) or sem
    for k in reads + writes:
        if k in BANKS:
            for q2, (j, wr) in S["b"].setdefault(k, {}).items():
                dep(j, q2 != q or (wr and k in reads))
    for k in reads:
        if k not in BANKS:
            for j in S["w"].get(k, []):
                dep(j, True)
    for k in writes:
        if k not in BANKS:
            for j in S["w"].get(k, []) + S["r"].get(k, []):
                dep(j, True)
    for k in reads + writes:
        if k in BANKS:
            acc = S["b"][k]
            acc[q] = (i, k in writes or (q in acc and acc[q][1] and k not in reads))
        elif k in writes:
            S["w"][k] = [i]
            S["r"][k] = []
    for k in reads:
        if k not in BANKS and k not in writes:
            S["r"].setdefault(k, []).append(i)
    S["ops"].append({"q": q, "cost": cost, "deps": deps, "fn": fn, "sig": sig, "lat": lat, "st": S.get("st", ""), "nm": " ".join(writes)})
    return i


def plan(S):
    ops = S["ops"]
    n = len(ops)
    succ = [[] for _ in range(n)]
    for i, o in enumerate(ops):
        for j in o["deps"]:
            succ[j].append(i)
    pri = [0.0] * n
    for i in range(n - 1, -1, -1):
        o = ops[i]
        b = 0.0
        for k in succ[i]:
            b = max(b, pri[k] + (o["lat"] if o["sig"] else (LAT if ops[k]["deps"][i] else 0.0)))
        pri[i] = b + o["cost"]
    pri = [p + BIAS.get(o["st"], 0.0) + BIAS.get(o["st"] + o["q"], 0.0) for p, o in zip(pri, ops)]
    left = [len(o["deps"]) for o in ops]
    ready = {}
    est = [0.0] * n
    free = {}
    for i in range(n):
        if left[i] == 0:
            ready.setdefault(ops[i]["q"], []).append(i)
    order = []
    end = 0.0
    while len(order) < n:
        best = None
        for q, lst in ready.items():
            if lst:
                st = max(free.get(q, 0.0), min(est[i] for i in lst))
                if best is None or st < best[0]:
                    best = (st, q)
        st, q = best
        lst = ready[q]
        c = max((i for i in lst if est[i] <= st + 1e-9), key=lambda i: (pri[i], -i))
        for i in lst:
            if pri[i] > pri[c] and est[i] < st + LOOK * ops[c]["cost"]:
                c = i
        st = max(st, est[c])
        lst.remove(c)
        o = ops[c]
        fin = st + o["cost"]
        free[q] = fin
        o["start"] = st
        end = max(end, fin + o["lat"])
        order.append(c)
        for k in succ[c]:
            d = ops[k]["deps"][c]
            l = o["lat"] if o["sig"] else (LAT if d else 0.0)
            est[k] = max(est[k], fin + l if d else st)
            left[k] -= 1
            if left[k] == 0:
                ready.setdefault(ops[k]["q"], []).append(k)
    S["end"] = end
    return order


def issue(S, order, eng, T):
    ops = S["ops"]
    cnt = {}
    known = {q: {} for q in eng}
    for i in order:
        o = ops[i]
        q = o["q"]
        kn = known[q]
        need = {}
        for j, sem in o["deps"].items():
            if sem:
                s, val = ops[j]["done"]
                if kn.get(s, 0) < val:
                    need[s] = max(need.get(s, 0), val)
        for s in sorted(need):
            eng[q].wait_ge(T.sem[s], need[s])
        for j, sem in o["deps"].items():
            if sem:
                for s, val in ops[j]["clock"].items():
                    if kn.get(s, 0) < val:
                        kn[s] = val
        if o["sig"]:
            o["fn"]()
            o["done"] = o["sig"]
        else:
            s = QSEM[q]
            cnt[s] = cnt.get(s, 0) + 1
            o["fn"]().then_inc(T.sem[s], 1)
            o["done"] = (s, cnt[s])
        o["clock"] = dict(kn)
        o["clock"][o["done"][0]] = o["done"][1]
    return cnt


def record(g, core, T, topo):
    rank = T.rank_of(core)
    S = {"ops": [], "w": {}, "r": {}, "b": {}, "sends": 0}
    v, sc, te = g.vector, g.scalar, g.tensor

    def seq(calls):
        def fn():
            for c in calls:
                x = c()
            return x
        return fn

    def V(cyc, R, W, *calls):
        return add(S, "v", max(cyc, 64 * len(calls)) * CYC, R, W, seq(calls))

    def SC(cyc, R, W, *calls):
        return add(S, "s", (cyc + SFIX * len(calls)) * CYC, R, W, seq(calls))

    def PE(cyc, R, W, mms):
        return add(S, "t", cyc * PEC, R, W, seq([(lambda m: lambda: te.matmul(*m))(m) for m in mms]))

    def G(cost, R, W, call):
        return add(S, "g", cost, R, W, call)

    def ts(out, in0, s1, s2, op0, op1=None):
        if op1 is None:
            return lambda: v.tensor_scalar(out, in0, s1, None, op0)
        return lambda: v.tensor_scalar(out, in0, s1, s2, op0, op1)

    def tt(out, a, b, op):
        return lambda: v.tensor_tensor(out, a, b, op)

    def cp(out, a):
        return lambda: v.tensor_copy(out, a)

    def ac(out, a, f, **kw):
        return lambda: sc.activation(out, a, f, **kw)

    def ms(ap, c):
        return lambda: v.memset(ap, c)

    def load(q, name, out, in_, W, lat):
        e = g.sync if q == "y" else g.scalar
        add(S, q, 0.06, [], W, lambda: e.dma_start(out, in_).then_inc(T.sem["ld_" + name], 16), ("ld_" + name, 16), lat)

    load("y", "fr", T.FI[:], T.front[:], ["FI"], 2.2)
    load("s", "v0", T.Z[:, 0:64], T.vein[:, 0:64], ["Z00"], 2.2)
    load("y", "wi", T.WI[:, 0:1], T.w[:], ["WI0"], 2.2)
    load("y", "li", T.WI[:, 1:2], T.lim[:], ["WI1"], 2.2)
    load("s", "v1", T.Z[:, 64:128], T.vein[:, 64:128], ["Z01"], 2.2)
    for b in range(4):
        load("y", "r%d" % b, T.ROCK[:, 1024 * b:1024 * b + 1024], T.rock[:, 1024 * b:1024 * b + 1024], ["ROCK%d" % b], 5.0)
    RK = ["ROCK%d" % b for b in range(4)]

    def ioF(ap, pat, base, cm):
        return lambda: g.iota(ap, pat, base, cm, allow_small_or_imprecise_dtypes=True)

    def ioI(ap, pat, base, cm):
        return lambda: g.iota(ap, pat, base, cm)
    G(0.15, [], ["PI"], ioI(T.PI[:, 0:1], [[1, 1]], 0, 1))
    G(0.35, [], ["GR"], ioF(T.GR[:], [[1, 8], [0, 16]], 0, 0))
    G(0.35, [], ["XR"], ioF(T.XR[:, 0:143], [[1, 143]], -15, 0))
    V(64, [], ["ONES"], ms(T.ONES[:], 1.0))
    G(0.45, ["ONES"], ["IEB"], lambda: g.affine_select(T.IEB[:, 0:158], T.ONES[:, 0:158], [[-1, 158]], A.is_equal, 0.0, 15, 1))
    G(0.35, [], ["CR"], ioF(T.CR[:], [[0, 8], [1, 16]], 0, 0))
    G(0.2, [], ["KM0"], ioF(T.KM16[:], [[1, 16]], 0, 0))
    V(64, ["PI"], ["PIr"], ts(T.PI[:, 1:2], T.PI[:, 0:1], 15, None, A.bitwise_and))
    V(64, ["PI"], ["PIg"], ts(T.PI[:, 2:3], T.PI[:, 0:1], 4, None, A.arith_shift_right))
    V(64, ["PIr"], ["r"], cp(T.RF[:, 0:1], T.PI[:, 1:2]))
    V(64, ["PIg"], ["gp"], cp(T.RF[:, 1:2], T.PI[:, 2:3]))
    r = T.RF[:, 0:1]
    gp = T.RF[:, 1:2]
    V(64, ["gp"], ["gp16"], ts(T.RF[:, 2:3], gp, 16.0, None, A.mult))
    V(128, ["GR", "gp"], ["BLK"], ts(T.BLK[:], T.GR[:], gp, None, A.is_equal))
    V(64, ["BLK"], ["BLH"], cp(T.BLH[:], T.BLK[:]))
    V(64, ["WI0"], ["WF0"], ts(T.WF[:, 0:1], T.WI[:, 0:1], 2.0, None, A.mult))
    V(64, ["WI1"], ["LIM"], ts(T.LIM[:], T.WI[:, 1:2], 0.5, None, A.add))
    V(64, ["LIM"], ["TOP0"], cp(T.TOP[:, 0:1], T.LIM[:]))
    V(64, ["BLK", "WF0"], ["W2"], ts(T.W2[:], T.BLK[:], T.WF[:, 0:1], None, A.mult))
    V(128, ["FI"], ["F00", "F01"], cp(T.F[:, 0:128], T.FI[:]))
    V(4 * 64, ["r"], ["BB"], *[ts(T.BB[:, m:m + 1], r, 37.0 * 2 ** (4 + m), 613.0 * m * 2 ** (4 + m), A.mult, A.add) for m in range(4)])
    V(64, ["r"], ["c1"], ts(T.RF[:, 4:5], r, -1.0, 1039.0, A.mult, A.add))
    V(64, ["r"], ["c2"], ts(T.RF[:, 5:6], r, -1.0, 1054.0, A.mult, A.add))
    V(64, ["PIr"], ["PIs"], ts(T.PI[:, 3:4], T.PI[:, 1:2], 1.0, None, A.add))
    V(64, ["PIs"], ["PIt"], ts(T.PI[:, 4:5], T.PI[:, 3:4], 15, None, A.bitwise_and))
    V(64, ["PIt"], ["rp1"], cp(T.RF[:, 3:4], T.PI[:, 4:5]))
    V(64, [], ["q25"], ms(T.RF[:, 6:7], 0.25))
    V(64, [], ["b129"], ms(T.RF[:, 8:9], 129.5))
    V(64, ["IEB"], ["NI"], ts(T.NI[:], T.IEB[:, 15:143], -1.0, None, A.mult))
    for n, c in (("R256", 256.0), ("R05", 0.5), ("R1B", 1.0), ("R1H", 1.0), ("R2H", 2.0)):
        V(143, ["XR", "gp16"], [n], ts(T[n][:, 0:143], T.XR[:, 0:143], T.RF[:, 2:3], c, A.is_equal, A.mult))
    V(64, [], ["ALLC"], ms(T.ALLC[:], 1.0 / 128))
    for h in range(2):
        for m in range(4):
            G(0.28, ["ONES"], ["K1%d%d" % (h, m)], (lambda h, m: lambda: g.affine_select(T.K1[:, h, 64 * m:64 * m + 64], T.ONES[:, 0:64], [[0, 64]], A.is_gt, 64.0 * m + (23 if m in NEARV[h] else 31), 0, 0))(h, m))
    V(80, ["IEB"], ["IEH"], cp(T.IEH[:, 0:158], T.IEB[:, 0:158]))
    V(128, ["IEB"], ["I32"], cp(T.I32[:], T.IEB[:, 15:143]))
    V(64, ["KM0", "r"], ["KT"], ts(T.KT[:], T.KM16[:], r, None, A.is_equal))
    V(512, [], ["W1"], ms(T.EX1[:], 1.0))
    for b in range(2):
        G(1.05, ["W1"], ["EX%d" % b], (lambda b: lambda: g.affine_select(T.EX[:, 512 * b:512 * b + 512], T.EX1[:], [[-1, 32], [0, 16]], A.is_equal, 0.0, -32 * b, 1))(b))
    V(64, [], ["NEG"], ms(T.NEG[:], -1.0))
    for l in range(16):
        G(0.4, ["NEG"], ["EL%d" % l], (lambda l: lambda: g.affine_select(T.EL[:, 128 * l:128 * l + 128], T.NEG[:], [[-16, 8], [0, 16]], A.is_equal, 0.0, -l, 1))(l))
        G(0.18, ["q25"], ["P4%d" % l], (lambda l: lambda: g.affine_select(T.P4[:, l:l + 1], T.RF[:, 6:7], [[0, 1]], A.is_gt, 4.0 ** l, 0, 0))(l))
    V(64, ["P4%d" % l for l in range(16)] + ["KT"], ["P4b"], tt(T.P4[:], T.P4[:], T.KT[:], A.mult))
    V(64, ["P4b"], ["P4C"], lambda: v.tensor_reduce(T.P4C[:], T.P4[:], AxisListType.X, A.add))
    V(64, ["BLK", "P4C"], ["Q2"], ts(T.Q2[:], T.BLK[:], T.P4C[:, 0:1], None, A.mult))
    V(128, ["CR", "r"], ["T32"], ts(T.T32[:], T.CR[:], r, -(2.0 ** 40), A.is_gt, A.mult))
    V(256, ["T32", "BLK"], ["SLB"], tt(T.SLB[:], T.T32[:], T.BLK[:], A.mult))
    for l in range(16):
        G(0.4, ["SLB"], ["PL%d" % l], (lambda l: lambda: g.affine_select(T.PL[:, 128 * l:128 * l + 128], T.SLB[:], [[-1, 128]], A.not_equal, 4.0 ** (15 - l), 0, 1))(l))
    V(128, ["CR", "r"], ["T32"], ts(T.T32[:], T.CR[:], r, None, A.is_ge))
    V(256, ["T32", "BLK"], ["UPI"], tt(T.UPI[:], T.T32[:], T.BLK[:], A.mult))
    V(64, ["ONES", "KT"], ["S15"], ts(T.S15[:], T.ONES[:, 0:128], T.KT[:, 15:16], None, A.mult))
    G(0.2, [], ["JCI0"], ioI(T.JCI[:, 0:8], [[16, 8]], 0, 0))
    V(64, ["JCI0", "r"], ["JCI1"], ts(T.JCI[:, 8:16], T.JCI[:, 0:8], r, None, A.add))
    V(64, ["JCI1"], ["PCH"], cp(T.PCH[:], T.JCI[:, 8:10]))
    V(64, ["JCI1"], ["DUMP"], ts(T.DUMP[:], T.JCI[:, 8:16], 4096.0, None, A.add))
    V(128, [], ["HWz0", "HWz1"], ms(T.HW0[:, 0:32], 0.0), ms(T.HW1[:, 0:32], 0.0))
    for t in range(NV):
        a = t + 1
        G(0.25, [], ["PRW%d" % t], ioF(T.PRW[:, 64 * t:64 * t + 64], [[1, 2 ** a], [2 ** a, 2 ** (6 - a)]], 0, 0))
        pc, pt, pf = T.PCI[:, 4 * t:4 * t + 4], T.PTI[:, 4 * t:4 * t + 4], T.PCF[:, 4 * t:4 * t + 4]
        V(64, ["JCI1"], ["PCI%d" % t], ts(pc, T.JCI[:, 8:12], 2 ** (6 - a) - 1, None, A.bitwise_and))
        V(64, ["JCI1"], ["PTI%d" % t], ts(pt, T.JCI[:, 8:12], 6 - a, None, A.arith_shift_right))
        V(64, ["PCI%d" % t], ["PCF%d" % t], ts(pf, pc, float(2 ** a), None, A.mult))
        V(64, ["PCF%d" % t, "PTI%d" % t], ["PCG%d" % t], tt(pf, pf, pt, A.add))
        V(256, ["PRW%d" % t, "PCG%d" % t], ["MK%d" % t],
          *[ts(T.MK[:, 256 * t + 64 * c:256 * t + 64 * c + 64], T.PRW[:, 64 * t:64 * t + 64], T.PCF[:, 4 * t + c:4 * t + c + 1], 8192.0, A.is_ge, A.mult) for c in range(4)])
    SC(0, ["q25"], ["lnw"], ac(T.RF[:, 7:8], T.RF[:, 6:7], AF.Ln))

    MM, EQ = T.MM, T.EQ
    IH = T.IEH[:, 15:143]
    PLK = ["PL%d" % l for l in range(16)]

    def claims(t, h):
        k, H, xk = "%d%d" % (t, h), str(h), "X%d" % h
        o = (2 * t + h) * 64
        F, Z, X = T.F[:, o:o + 64], T.Z[:, o:o + 64], T[xk]
        CO, ZX = T["CO" + H], T["ZX" + H]
        nX = X[:, 384:448]
        SC(5 * 64, ["F" + k, "BB"], [xk], ac(nX, F, AF.Copy),
           *[ac(X[:, 128 + 64 * m:192 + 64 * m], F, AF.Identity, bias=T.BB[:, m:m + 1], scale=float(2 ** (4 + m))) for m in range(4)])
        PE(128, ["Z" + k, "W2", "BLK"], [xk], [(X[:, 0:64], T.W2[:], Z, True, True), (X[:, 64:128], T.BLK[:], Z, True, True)])
        hh, u1 = T.UA[:, h, 0:64], T.UI[:, h, :]
        V(128, [xk], ["UA" + H], ts(T.UA[:, h, :], X[:, 0:128], 1.0, None, A.add))
        V(64, ["UA" + H], ["UI" + H], ts(u1, hh, 4095, None, A.bitwise_and))
        V(64, [xk, "UI" + H], ["QI" + H], tt(T.QI[:, h, :], nX, u1, A.mult))
        V(64, ["QI" + H], ["UAh" + H], ts(hh, T.QI[:, h, :], 1, None, A.arith_shift_right))
        V(256, [xk, "UAh" + H], ["HM" + H], *[tt(T.HM[:, h, 64 * m:64 * m + 64], X[:, 128 + 64 * m:192 + 64 * m], hh, A.add) for m in range(4)])
        V(256, ["HM" + H], ["C4" + H], *[ts(T.C4[:, h, 64 * m:64 * m + 64], T.HM[:, h, 64 * m:64 * m + 64], 4 + m, 4095, A.arith_shift_right, A.bitwise_and) for m in range(4)])
        V(256, ["C4" + H], ["CO" + H], cp(CO[:], T.C4[:, h, :]))
        if ZXP[h]:
            PE(128, ["Z" + k, "IEB"], ["HA"], [(T.HA[0:64, 0:128], Z, T.IEB[:, 15:143], True, True)])
            SC(128, ["HA"], ["ZT" + H], ac(T.ZT[0:64, h, :], T.HA[0:64, 0:128], AF.Copy))
            for b, bk in ((0, "HB"), (1, "HA")):
                PE(512, ["ZT" + H, "EX0", "EX1"], [bk], [(T[bk][:], T.ZT[0:64, h, :], T.EX[0:64, 512 * b:512 * b + 512], True, True)])
                SC(512, [bk], ["ZX%s%d" % (H, 8 * b), "ZX%s%d" % (H, 8 * b + 4)], ac(ZX[:, 512 * b:512 * b + 512], T[bk][:], AF.Copy))
        else:
            for b in range(0, 16, 4):
                if b < ZXV[h]:
                    V(256, ["Z" + k], ["ZX%s%d" % (H, b)], *[cp(ZX[:, p:1024:16], Z) for p in range(b, b + 4)])
                else:
                    SC(256, ["Z" + k], ["ZX%s%d" % (H, b)], *[ac(ZX[:, p:1024:16], Z, AF.Copy) for p in range(b, b + 4)])
        V(64, ["UA" + H], ["SI" + H], ts(T.SI[:, h, :], T.UA[:, h, 64:128], 15, None, A.bitwise_and))
        V(256, [xk, "C4" + H], ["DN" + H], *[tt(T.DN[:, h, 64 * m:64 * m + 64], T.C4[:, h, 64 * m:64 * m + 64], nX, A.subtract) for m in range(4)])
        V(64, ["UI" + H], ["UF" + H], ts(T.UF[:, h, :], T.UI[:, h, 1:64:2], -1.0, 0.5, A.add, A.mult))
        V(128, ["SI" + H, "rp1"], ["SM" + H], *[ts(T.SM[:, h, 32 * b:32 * b + 32], T.SI[:, h, b:64:2], T.RF[:, 3:4], None, A.is_equal) for b in range(2)])
        zb = T.ZB[:, h, :]
        SC(64, ["Z" + k], ["ZB" + H], *[ac(T.ZB[:, h, 32 * b:32 * b + 32], T.Z[:, o + b:o + 64:2], AF.Copy) for b in range(2)])
        SC(64, ["ZB" + H], ["Z5" + H], ac(T.Z5[:, h, :], zb, AF.Copy, bias=-0.5))
        SC(64, ["ZB" + H], ["Z4" + H], ac(T.Z4[:, h, :], zb, AF.Copy, scale=0.25, bias=129 - 0.375))
        PE(128, ["ZB" + H, "Z4" + H, "IEB"], [xk], [(X[:, 0:64], T.IEB[:, 15:143], T.Z4[:, h, :], True, False), (X[:, 0:64], T.IEB[:, 15:143], zb, False, True)])
        PE(256, ["F" + k, "I32"], [xk], [(X[:, 448:512], T.I32[:], F, True, False)])

    def moves(t, h):
        k, H = "%d%d" % (t, h), str(h)
        kk = BANKS[2 + h]
        KK = T[kk]
        CO, ZX = T["CO" + H], T["ZX" + H]
        o = (2 * t + h) * 64
        for m in range(4):
            d, n = "D%d%d" % (h, m), "N%d%d" % (h, m)
            dm, nm = T.D[:, h, 1024 * m:1024 * m + 1024], T.NR[:, h, 1024 * m:1024 * m + 1024]
            zk = ["ZX%s%d" % (H, b) for b in range(0, 16, 4)]
            win = T.ROCK[:, 0:4096].indirect(CO[:, 64 * m:64 * m + 64])
            if m in SG:
                xg = T["XG" + H]
                SC(1536, RK + ["CO" + H], ["XG" + H], ac(xg[:], win, AF.Copy))
                for b, bk in ((0, "HA"), (1, "HB")):
                    PE(1024, ["XG" + H, "IEB", "NI"] + zk, [bk], [(T[bk][:], T.IEB[:, 15:143], xg[:, 512 * b:512 * b + 512], True, False),
                                                                (T[bk][:], T.NI[:], ZX[:, 512 * b:512 * b + 512], False, True)])
                    SC(512, [bk], [d + "ab"[b]], ac(T.D[:, h, 1024 * m + 512 * b:1024 * m + 512 * b + 512], T[bk][:], AF.Abs))
            else:
                V(60 + 1536, RK + ["CO" + H] + zk, [d + "a", d + "b"], tt(dm, win, ZX[:], A.subtract))
                SC(1024, [d + "a", d + "b"], [d + "a", d + "b"], ac(dm, dm, AF.Abs))
            if m in NEARV[h]:
                V(512, [d + "a", d + "b", "TOP%d" % t], [n + "a", n + "b"], ts(nm, dm, T.TOP[:, t:t + 1], None, A.is_le))
            else:
                SC(1024, [d + "a", d + "b", "TOP%d" % t], [n + "a", n + "b"], ac(nm, dm, AF.Sign, bias=T.TOP[:, t:t + 1], scale=-1.0))

        def keys(m, near):
            w, src, b = (("R1B" if m in NEARV[h] else "R05"), T.NR, "N") if near else ("R256", T.D, "D")
            PE(1024, ["%s%d%d%s" % (b, h, m, x) for x in "ab"] + [w], [kk], [(KK[:, 64 * m:64 * m + 64], T[w][:, 15 - p:143 - p], src[:, h, 1024 * m + p:1024 * m + 1024:16], False, near and m % 2 == 1 and p == 15) for p in range(16)])
        for b in (0, 1):
            PE(128, ["ALLC"] + ["K1%d%d" % (h, m) for m in range(4)], [kk], [(KK[:, 128 * b:128 * b + 128], T.ALLC[:], T.K1[:, h, 128 * b:128 * b + 128], True, False)])
            for m, near in ((0, 0), (1, 0), (0, 1), (1, 1)):
                keys(2 * b + m, bool(near))
            if b == 0:
                SC(128, [kk], ["KS" + H], ac(T.KS[:, h, :], KK[:, 0:128], AF.Copy))
        V(128, [kk, "KS" + H], ["KM" + H], tt(T.KM[:, h, :], KK[:, 128:256], T.KS[:, h, :], A.min))
        V(128, ["KM" + H], ["KB" + H], tt(T.KB[:, h, :], T.KM[:, h, 0:64], T.KM[:, h, 64:128], A.min))
        V(64, ["KB" + H], ["KC" + H], ts(T.KC[:, h, :], T.KB[:, h, :], 255, 5, A.bitwise_and, A.arith_shift_right))
        V(256, ["KC" + H], [kk], *[ts(KK[:, 256 + 64 * m:320 + 64 * m], T.KC[:, h, :], float(2 * m + 1), None, A.is_equal) for m in range(4)])
        V(256, [kk, "DN" + H], ["PR" + H], tt(T.PR[:, h, :], KK[:, 256:512], T.DN[:, h, :], A.mult))
        X = T["X" + H]
        PE(4 * 256, ["PR" + H, "I32"], ["X" + H], [(X[:, 448:512], T.I32[:], T.PR[:, h, 64 * m:64 * m + 64], False, m == 3) for m in range(4)])

    def meetings(t, h):
        k, H = "%d%d" % (t, h), str(h)
        o = (2 * t + h) * 64
        kk, xk = BANKS[2 + h], "X" + H
        KK, NP = T[kk], T[xk][:, 448:512]
        HW, LS, FO = T["HW" + H], T["LS" + H], T.FO
        SS, JJ = T.NS[:, h, 0:64:2], T.NS[:, h, 1:64:2]
        V(64, [xk], ["HF" + H], ts(T.HF[:, h, :], NP, 0.125, 1025 - 0.4375, A.mult, A.add))
        V(64, [xk], ["JC" + H], ts(T.JC[:, h, 0:32], T[xk][:, 449:512:2], -2048.0, None, A.add))
        V(64, [xk], ["JS" + H], ts(T.JC[:, h, 32:64], T[xk][:, 448:512:2], -1.0, 2048.0, A.mult, A.add))
        SC(64, [xk], ["NS" + H], ac(T.NS[:, h, :], NP, AF.Copy))
        SC(64, ["NS" + H], ["S2" + H], ac(T.S2[:, h, :], T.NS[:, h, :], AF.Copy, bias=-2048.0))
        for b, bk in ((0, "EQ"), (1, "MM")):
            mm = []
            for l in range(8):
                dd = T[bk][:, 32 * l:32 * l + 32]
                mm.append((dd, IH, T.HF[:, h, 1:64:2], True, False))
                mm.append((dd, T.EL[:, 128 * (8 * b + l):128 * (8 * b + l) + 128], T.HF[:, h, 0:64:2], False, True))
            PE(16 * 64, ["HF" + H, "IEH"] + ["EL%d" % l for l in range(16)], [bk], mm)
            V(256, [bk], ["EQB%s%d" % (H, b)], ts(T.EQB[:, h, 256 * b:256 * b + 256], T[bk][:, 0:256], 0.0, None, A.is_equal))
            PE(512, ["EQB%s%d" % (H, b)] + PLK, [kk], [(KK[:, 256:288], T.PL[:, 128 * l:128 * l + 128], T.EQB[:, h, 32 * l:32 * l + 32], l == 0, l == 15) for l in range(8 * b, 8 * b + 8)])
        pm = T.PM[:, h, :]
        for bk, s0, s1 in [("HA" if x < 16 else "HB", max(x, 1), x + 4) for x in range(0, 32, 4)]:
            mm = []
            for s in range(s0, s1):
                dd = T[bk][:, 32 * (s % 16):32 * (s % 16) + 32]
                mm += [(dd, T.IEH[:, s - 1:s + 127], T.JC[:, h, 0:32], True, False), (dd, IH, T.JC[:, h, 32:64], False, True)]
            PE(64 * len(mm), ["JC" + H, "JS" + H, "IEH"], [bk], mm)
        V(64, [kk], ["PM" + H], ts(pm, KK[:, 256:288], 0.0, None, A.max))
        PE(192, ["PM" + H, "Q2", "BLK", "UPI"], [kk], [(KK[:, 288:320], T.Q2[:], pm, True, True), (KK[:, 320:352], T.BLK[:], pm, True, True),
                                                       (KK[:, 352:384], T.UPI[:], pm, True, True)])
        SC(64, [kk, "lnw"], ["LN" + H], ac(T.LN[:, h, :], KK[:, 288:352], AF.Ln, bias=T.RF[:, 6:7]))
        SC(480, ["HA"], ["HWa" + H], ac(HW[:, 32:512], T.HA[:, 32:512], AF.Copy))
        SC(512, ["HB"], ["HWb" + H], ac(HW[:, 512:1024], T.HB[:, 0:512], AF.Copy))
        V(64, ["LN" + H], ["XX" + H], ts(T.XX[:, h, :], T.LN[:, h, :], 1.0 / math.log(4.0), 1024.0, A.mult, A.add))
        V(64, [kk], ["JM" + H], ts(T.JM[:, h, :], KK[:, 352:384], 0.0, None, A.is_gt))
        PE(17 * 64, ["XX" + H, "R2H", "PCH", "IEH"], [kk], [(KK[:, 128:130], IH, T.PCH[:], True, False)] +
           [(KK[:, 128:130], T.R2H[:, 15 - p:143 - p], T.XX[:, h, p:32:16], False, p == 15) for p in range(16)])
        ji, ju, dj = T.JI[:, h, :], T.JU[:, h, :], T.DJ[:, h, :]
        V(64, ["NS" + H], ["JI" + H], tt(ji, JJ, SS, A.mult))
        V(64, ["NS" + H, "UF" + H], ["JU" + H], tt(ju, JJ, T.UF[:, h, :], A.add))
        V(64, ["JI" + H], ["JI" + H], ts(ji, ji, 5, None, A.arith_shift_right))
        V(64, ["JI" + H, "JU" + H], ["JU" + H], tt(ju, ji, ju, A.add))
        V(64, ["JU" + H], ["JU" + H], ts(ju, ju, 4095, None, A.bitwise_and))
        V(64, ["JU" + H, "NS" + H], ["DJ" + H], tt(dj, ju, JJ, A.subtract))
        V(64, ["DJ" + H, "JM" + H], ["DJ" + H], tt(dj, dj, T.JM[:, h, :], A.mult))
        V(64, ["DJ" + H, "S2" + H], ["FCj" + H], tt(T.FC[:, h, 32:64], dj, T.S2[:, h, 1:64:2], A.add))
        SC(32, ["FCj" + H], ["FOj" + k], ac(FO[:, o + 32:o + 64], T.FC[:, h, 32:64], AF.Copy, bias=2048.0))
        jg = T.JG[:, h, :]
        V(64, ["XX" + H, "c1"], ["CDa" + H], ts(T.CD[:, h, 0:32], T.XX[:, h, 32:64], T.RF[:, 4:5], None, A.is_gt))
        V(64, ["XX" + H, "c2"], ["CDb" + H], ts(T.CD[:, h, 32:64], T.XX[:, h, 0:32], T.RF[:, 5:6], None, A.is_le))
        V(64, ["CDa" + H, "CDb" + H], ["CD" + H], tt(T.CD[:, h, 64:96], T.CD[:, h, 0:32], T.CD[:, h, 32:64], A.mult))
        V(64, [kk], ["LS" + H], ts(LS[:], KK[:, 128:130], -32.0 * 1023, None, A.add))
        V(110, ["LS" + H, "CD" + H, "HWz" + H, "HWa" + H, "HWb" + H], ["JG" + H], tt(jg, HW[:].indirect(LS[:]), T.CD[:, h, 64:96], A.mult))
        V(64, ["JG" + H, "S2" + H], ["FCs" + H], tt(T.FC[:, h, 0:32], jg, T.S2[:, h, 0:64:2], A.add))
        SC(32, ["FCs" + H], ["FOs" + k], ac(FO[:, o:o + 32], T.FC[:, h, 0:32], AF.Copy, bias=2048.0))

    def send(kind, t, h, R):
        if t == NV - 1:
            return
        dst = T.cores[(rank + 3) % 8]
        rid, pid, _ = topo.addr(dst)
        n, mask = len(topo.engines(core, dst)), topo.mask(core, dst)
        o = (2 * t + h) * 64
        src, out = (T.FO, T.F) if kind == "f" else (T.ZO, T.Z)
        sem = "ar%s%d%d" % (kind, t + 1, h)
        add(S, "g", 0.1, R, [("F" if kind == "f" else "Z") + "%d%d" % (t + 1, h)],
            lambda: g.remote_dma(out[:, o + 128:o + 192], src[:, o:o + 64], T.sem[sem], T.sem.sl, pid, rid, mask), (sem, n), 2.2)
        S["sends"] += n

    def mining(t, h):
        k, H = "%d%d" % (t, h), str(h)
        o = (2 * t + h) * 64
        MF, E16 = T.MF, T["E16" + H]
        ef = T.EF[:, h, 0:4]
        send("f", t, h, ["FOj" + k, "FOs" + k])
        V(128, ["FCj" + H, "FCs" + H, "SM" + H], ["MF" + H], tt(MF[:, 64 * h:64 * h + 64], T.FC[:, h, :], T.SM[:, h, :], A.mult))
        kk, bk = BANKS[2 + h], ("MM", "EQ")[h]
        KK, DD = T[kk], T[bk]
        PE(1024, ["MF" + H, "R1H"], [kk], [(KK[:, 160:164], T.R1H[:, 15 - p:143 - p], MF[:, 64 * h + p:64 * h + 64:16], p == 0, p == 15) for p in range(16)])
        V(64, [kk], ["E16" + H], ts(E16[:], KK[:, 160:164], 2048.0, None, A.add))
        V(64, [kk], ["EF" + H], cp(ef, KK[:, 160:164]))
        SC(4, [kk], ["EG" + H], ac(T.EF[:, h, 4:8], KK[:, 160:164], AF.Copy, bias=2048.0))
        su = T.SU[:, h, :]
        V(156, RK + ["E16" + H, "Z5" + H], ["SU" + H], tt(su, T.ROCK[:, 0:4096].indirect(E16[:]), T.Z5[:, h, :], A.add))
        V(64, ["SU" + H], ["Y1" + H], ts(T.Y1[:, h, :], su, 0.5, None, A.mult))
        V(64, ["Y1" + H], ["ZO" + k], cp(T.ZO[:, o:o + 64], T.Y1[:, h, :]))
        send("z", t, h, ["ZO" + k])
        w = 64 + 64 * h
        mm = []
        for c in range(4):
            mm.append((DD[:, c * w:c * w + w], T.BLH[:], MF[:, 0:w], True, False))
            mm.append((DD[:, c * w + w - 64:c * w + w], IH, T.MK[:, 256 * t + 64 * c:256 * t + 64 * c + 64], False, True))
        PE(4 * w + 256, ["MF0", "MF" + H, "MK%d" % t, "BLH", "IEH"], [bk], mm)
        for c in range(4):
            du = T.DU[:, h, c * w:c * w + w]
            V(w, [bk, "EF" + H], ["DU%s%d" % (H, c)], ts(du, DD[:, c * w:c * w + w], T.EF[:, h, c:c + 1], 8192.0, A.is_equal, A.mult))
            j = 4 * h + c
            lo = T.LO[:, j:j + 1]
            if c in LOV[h]:
                V(w, ["DU%s%d" % (H, c)], ["LO%s%d" % (H, c)], (lambda lo, du: lambda: v.tensor_reduce(lo, du, AxisListType.X, A.add))(lo, du))
            else:
                SC(w + 24, ["DU%s%d" % (H, c)], ["DU%s%d" % (H, c), "LO%s%d" % (H, c)], ac(du, du, AF.Copy, accum_out=lo))
            V(64, ["LO%s%d" % (H, c), "DUMP", "EG" + H], ["OF%d" % j], ts(T.OF[:, j:j + 1], lo, T.DUMP[:, j:j + 1], T.EF[:, h, 4 + c:5 + c], A.min, A.max))
        V(64, ["SU" + H, "X" + H], ["RR" + H], tt(T.RR[:, h, :], su, T["X" + H][:, 0:64], A.subtract))
        SC(64, ["RR" + H, "b129"], ["RN" + H], ac(T.RN[:, 64 * h:64 * h + 64], T.RR[:, h, :], AF.Relu, bias=T.RF[:, 8:9]))

    names = [(claims, "c"), (moves, "m"), (meetings, "e"), (mining, "i")]

    def stage(f, t, h):
        S["st"] = [n for f2, n in names if f2 == f][0] + str(h)
        f(t, h)
        S["st"] = ""

    for t in range(NV):
        stage(claims, t, 0)
        if t == 0:
            stage(claims, t, 1)
        stage(moves, t, 0)
        if t > 0:
            stage(claims, t, 1)
        stage(moves, t, 1)
        stage(meetings, t, 0)
        stage(meetings, t, 1)
        stage(mining, t, 0)
        stage(mining, t, 1)
        V(60 + 128 * 3.8, ["OF%d" % j for j in range(8)] + ["RN0", "RN1"], RK, cp(T.ROCK[:].indirect(T.OF[:]), T.RN[:]))
        if t < NV - 1:
            PE(128, ["JM0", "JM1", "S15"], ["MM"], [(MM[:, 256 + 32 * h:288 + 32 * h], T.S15[:], T.JM[:, h, :], True, True) for h in range(2)])
            V(64, ["MM"], ["CN"], lambda: v.tensor_reduce(T.CN[:, 0:1], MM[:, 256:320], AxisListType.X, A.add))
            V(64, ["CN"], ["CI0"], cp(T.CI[:, 0:1], T.CN[:, 0:1]))
            V(64, ["CI0"], ["CI1"], ts(T.CI[:, 1:2], T.CI[:, 0:1], 3, None, A.bitwise_and))
            V(64, ["CI1", "LIM"], ["TOP%d" % (t + 1)], ts(T.TOP[:, t + 1:t + 2], T.CI[:, 1:2], T.LIM[:, 0:1], None, A.add))
    t = NV - 1
    for h in range(2):
        o = (2 * t + h) * 64
        for b in range(2):
            c = 64 * h + 32 * b
            SC(32, ["FOj%d%d" % (t, h), "FOs%d%d" % (t, h)], ["YF%d%d" % (h, b)], ac(T.YF[:, c:c + 32], T.FO[:, o + b:o + 64:2], AF.Copy))
            SC(32, ["ZO%d%d" % (t, h)], ["YZ%d%d" % (h, b)], ac(T.YZ[:, c:c + 32], T.ZO[:, o + b:o + 64:2], AF.Copy))
    hb = ["00", "01", "10", "11"]
    add(S, "y", 0.06, ["YF" + x for x in hb], ["oF"], lambda: g.sync.dma_start(T.yf[:], T.YF[:]).then_inc(T.sem.od_f, 16), ("od_f", 16), 2.0)
    add(S, "y", 0.06, ["YZ" + x for x in hb], ["oZ"], lambda: g.sync.dma_start(T.yz[:], T.YZ[:]).then_inc(T.sem.od_z, 16), ("od_z", 16), 2.0)
    add(S, "y", 0.06, RK, ["oX"], lambda: g.sync.dma_start(T.yx[:], T.ROCK[:, 0:4096]).then_inc(T.sem.od_x, 16), ("od_x", 16), 5.0)
    return S


def rank_program(g, core, T, topo):
    if T.rank_of(core) is None:
        return
    S = record(g, core, T, topo)
    order = plan(S)
    eng = {"v": g.vector, "s": g.scalar, "t": g.tensor, "g": g, "y": g.sync}
    cnt = issue(S, order, eng, T)
    for s in sorted(cnt):
        g.wait_ge(T.sem[s], cnt[s])
    for s in ("od_f", "od_z", "od_x"):
        g.wait_ge(T.sem[s], 16)
    g.wait_ge(T.sem.sl, S["sends"])
